import numpy as np, ml_dtypes
CORES = [3,11,19,27,35,43,51,59]
N = 8
import mx_ref
BF = ml_dtypes.bfloat16
def pick(q, e):
    c = np.concatenate([q[0].reshape(128, -1, 4), np.zeros((128, 1, 4), np.uint8)], axis=1); s = np.concatenate([q[1], np.ones((16, 1), np.uint8)], axis=1)
    return (np.ascontiguousarray(c[:, e].reshape(128, -1)), np.ascontiguousarray(s[:, e]))
def join(*qs):
    return (np.concatenate([q[0] for q in qs], axis=1), np.concatenate([q[1] for q in qs], axis=1))
def put(q, e, v):
    c, s = q[0].reshape(128, -1, 4).copy(), q[1].copy(); c[:, e] = v[0].reshape(128, -1, 4); s[:, e] = v[1]
    return (c.reshape(128, -1), s)
def pk(c, s):
    return (np.ascontiguousarray(c), mx_ref.live(s))
def emit(q):
    return q[0], q[1]
def tile(rs):
    return np.stack(rs, axis=2).reshape(128, -1).astype(BF)
def f(rng, *shape):
    return mx_ref.flush((rng.standard_normal(shape, dtype=np.float32) * np.exp2(rng.integers(-2, 3, shape[:-1] + (1,)))).astype(BF))
def wide(rng, *shape, cols=0):
    v = rng.standard_normal(shape, dtype=np.float32) * np.exp2(rng.integers(-12, 13, shape)).astype(np.float32)
    if cols: v *= np.repeat(np.exp2(rng.integers(-cols, cols + 1, shape[:-2] + (1, shape[-1] // 4))) * (rng.random(shape[:-2] + (1, shape[-1] // 4)) > 0.0625), 4, axis=-1).astype(np.float32)
    return mx_ref.flush(v.astype(BF))
P, K, CAPP, R, L, B = 128, 16, 8, 3, 3, 10
def falling(s):
    return np.argsort(-(s + np.float32(0)), kind="stable")
def bits(g, first, n):
    return np.sum([(g[first + i] > 0) * 2 ** i for i in range(n)], axis=0)
def astile(v):
    s, n = v.shape[:-2], v.shape[-1]
    return np.ascontiguousarray(np.swapaxes(v.reshape(s + (128, 4, n)), -1, -2)).reshape(s + (128, 4 * n))
def weigh(rng, t):
    c, s = mx_ref.quantize(np.ascontiguousarray(t))
    p = mx_ref.plane(s, rng)
    return {"wc": np.stack([c] * N), "ws": np.stack([p] * N)}
def steer(rng, sign, low, at, free, same=False, xs=1.0, us=2.0 ** 13, lean=None):
    v = np.zeros((N, 512, P), np.float32)
    v[:, :128] = np.where(sign < 0, 112, 0)[:, None, :]
    v[:, 128:256] = np.where(sign > 0, 112, 0)[:, None, :]
    for t in range(3):
        for k in range(3): v[:, 256 + 3 * t + k] = low[t] // 8 ** k % 8
    if lean is not None: v[:, 265:266 + B] = lean
    for k in range(4):
        for i in range(L):
            one = at[:, :, k] // 2 ** i % 2
            v[:, 288 + 8 * k + 2 * i] = one
            v[:, 289 + 8 * k + 2 * i] = 1 - one
    v[:, 320:] = free
    a = np.zeros((2, 512, 512), np.float32)
    for m in range(2):
        j = np.arange(256)
        a[m, j, j] = 20
        j = np.arange(9)
        a[m, 256 + j, 256 + (j + 3) % 9] = 20
        j = np.arange(265, 265 + B)
        a[m, j, j] = 20
        a[m, 280 + 4 * m, 265 + B] = 20
        j = np.arange(32)
        a[m, 288 + j, 288 + (j + 8 * (m + 1)) % 32] = 20
        a[m, 320:, 320:] = rng.standard_normal((192, 192))
        if same and m == 0: a[m, 320:, 320:] = 20 * np.eye(192)
    w = np.concatenate([astile(np.ascontiguousarray(a[m][b::4].T)) for m in range(2) for b in range(4)], axis=1)
    h = np.zeros((512, 128), np.float32)
    h[:128, 0] = -448
    h[128:256, 0] = 448
    h[256:259, 0] = [1, 8, 64]
    for i in range(L):
        h[288 + 2 * i, 1 + i] = 1
        h[289 + 2 * i, 1 + i] = -1
    for i in range(B):
        h[265 + i, 1 + L + i] = 256
        h[265 + i, 1 + L + (i + 1) % B] = -256
    h[280, 1 + L:1 + L + B] = -256
    h[284, 1 + L:1 + L + B] = 256
    k = rng.standard_normal((192, B))
    h[320:, 1 + L:1 + L + B] = k - np.mean(k, axis=0)
    h[:, 1 + L + B:] = rng.standard_normal((512, 127 - L - B))
    x = mx_ref.flush((astile(v) * np.float32(xs)).astype(BF))
    u = mx_ref.flush((astile(h) * np.float32(us)).astype(BF))
    return {"x": x, "u": np.stack([u] * N), **weigh(rng, mx_ref.flush(w.astype(BF)))}
def setup_inputs(rng):
    return {"x": f(rng, N, 128, 4 * P), "u": np.stack([f(rng, 128, 512)] * N), **weigh(rng, f(rng, 128, 4096))}
def setup_inputs_close(rng):
    low = rng.integers(0, P // 2 - 1, (3, N, P))
    low[0] = P // 2 + (np.arange(P) + 1) // 2
    best = np.argsort(-low[0, 0], kind="stable")
    low[1][:, best[R * K - 1]] = P // 2 - 1
    at, free = rng.integers(0, N, (N, P, 4)), rng.standard_normal((N, 192, P))
    free[:, :, best[R * K:]] = 0
    lean = np.zeros((N, B + 1, P))
    for r in range(N):
        lean[r, rng.integers(0, B, R * K), best[:R * K]] = 1
        for t in range(R):
            to, e = rng.permutation(np.arange(2 * K) % N), best[t * K:t * K + K]
            at[r, e, 1], at[r, e, 2] = to[0::2], to[1::2]
    z, s = [int(k) for k in np.sort(rng.permutation(N)[:2])]
    for r in (z, s):
        low[1, r, best[0]] = P // 2 - 1
        free[r, :, best[0]] = 0
        lean[r, :, best[0]] = 0
    lean[s, B, best[0]] = 1
    return steer(rng, np.full((N, P), -1), low, at, free, lean=lean)
def setup_inputs_ties(rng):
    n, own = P // 4, K // 4
    def some(*shape):
        return rng.integers(4, 8, shape) * np.exp2(rng.integers(-1, 2, shape)) * (rng.random(shape) < 0.25)
    low, at, free = rng.integers(0, 4, (3, n)), rng.integers(0, N, (n, 4)), some(192, n)
    low[0] = np.arange(n) % 2
    e = np.stack([rng.permutation(np.arange(P) % n) for r in range(N)])
    lows, ats = low[:, e], at[e]
    frees = np.stack([free[:, e[r]] for r in range(N)])
    none = []
    for r in range(N):
        p = rng.permutation(P)
        k = p[:own]
        none.append(p[own:own + 2])
        lows[0, r, k], lows[1, r, k] = 2, 400
        ats[r, k] = rng.integers(0, N, (own, 4))
        ats[r, k, 1], ats[r, k, 2] = r, (r + 1) % N
        frees[r][:, k] = some(192, own)
    d = steer(rng, np.full((N, P), -1), lows, ats, frees, same=True)
    x, u = np.array(d["x"]), np.array(d["u"])
    for r in 1 + rng.permutation(N - 1)[:2]:
        for j in none[r]: x[r, :, 4 * j:4 * j + 4] = 0
    u[:, 80:, 4 * (1 + L):4 * (2 + L)] = np.abs(u[:, 80:, 4 * (1 + L):4 * (2 + L)].astype(np.float32)).astype(BF)
    return {**d, "x": x, "u": u}
def setup_inputs_crowd(rng):
    a, b, c, d = [int(k) for k in rng.permutation(N)[:4]]
    low = np.stack([np.stack([rng.permutation(P) for r in range(N)])] * 3)
    low[1] = 2 * P - low[0]
    low[2] = rng.integers(400, 500, (N, P))
    at, free = rng.integers(0, N, (N, P, 4)), rng.standard_normal((N, 192, P))
    for r in range(N):
        to = rng.choice(np.delete(np.arange(N), d), 2 * K)
        if r == a or r == b: to[:] = b
        elif r == c:
            to[:] = c
            to[:CAPP] = b
            to[CAPP:2 * CAPP + 1] = a
        else: to[:CAPP + int(rng.integers(1, 3))] = b
        to = rng.permutation(to)
        top = np.argsort(-low[0, r], kind="stable")[:K]
        at[r, top, 1], at[r, top, 2] = to[0::2], to[1::2]
    top = np.argsort(-low[0, a], kind="stable")[:K]
    e = top[:CAPP // 2]
    low[1, a, top[CAPP // 2:]] += P - K
    for t in range(3): low[t, a, e] = low[t, a, e[0]]
    at[a, e] = at[a, e[0]]
    free[a][:, e] = free[a][:, e[:1]]
    return steer(rng, np.full((N, P), -1), low, at, free)
def setup_inputs_huge(rng):
    sign = np.full((N, P), -1)
    for r in rng.permutation(N)[:N // 2]: sign[r, rng.permutation(P)[:K // 2]] = 1
    return steer(rng, sign, rng.integers(0, 512, (3, N, P)), rng.integers(0, N, (N, P, 4)), rng.standard_normal((N, 192, P)), xs=2.0 ** 23, us=2.0 ** 21)
def setup_inputs_spread(rng):
    return {**setup_inputs(rng), "x": wide(rng, N, 128, 4 * P, cols=6)}
def check_inputs(d):
    b = []
    for k in ("x", "u"):
        v = np.abs(d[k].astype(np.float32))
        if not (np.isfinite(v).all() and ((v == 0) | (v >= 2.0 ** -30) & (v <= 2.0 ** 30)).all()): b.append("a value of " + k)
    for k in ("u", "wc", "ws"):
        v = d[k].astype(np.float32)
        if (v != v[:1]).any(): b.append(k + " is not the same on every rank")
    if ((d["wc"] & 127) == 127).any(): b.append("a code of wc")
    zero, least, most = [int(mx_ref.quantize(np.full((128, 16), k, np.float32).astype(BF))[1].max()) for k in (0.0, 2.0 ** -30, 2.0 ** 30)]
    for r in range(N):
        s = mx_ref.live(d["ws"][r]).astype(int)
        if ((s != zero) & ((s < least) | (s > most))).any():
            b.append("a scale of ws")
            break
    return b
def reference(x, u, wc, ws):
    y, oc, osc = np.zeros((N, 128, R * P), np.float32), np.zeros((N, 128, 4 * P), np.uint8), np.zeros((N, 16, P), np.uint8)
    held = [mx_ref.quantize(np.ascontiguousarray(x[r])) for r in range(N)]
    qu = [mx_ref.quantize(np.ascontiguousarray(u[r])) for r in range(N)]
    w = []
    for r in range(N):
        q = pk(wc[r], ws[r])
        w.append([pick(q, np.arange(128 * i, 128 * i + 128)) for i in range(8)])
    for t in range(R):
        g = [mx_ref.matmul(qu[r], held[r]) for r in range(N)]
        top = [falling(g[r][0])[:K] for r in range(N)]
        kids, to = [], []
        for r in range(N):
            v = pick(held[r], top[r])
            z = [mx_ref.matmul(w[r][i], v) for i in range(8)]
            rs = [np.stack([z[b], z[4 + b]], axis=2).reshape(128, -1) for b in range(4)]
            kids.append(mx_ref.quantize(tile([np.maximum(e, np.float32(0)) * np.float32(0.05) for e in rs])))
            to.append(bits(mx_ref.matmul(qu[r], kids[r]), 1, L))
        for q in range(N):
            e = np.full((N, CAPP), -1)
            for r in range(N):
                k = np.flatnonzero(to[r] == q)[:CAPP]
                e[r, :len(k)] = k
            came = join(*[pick(kids[r], e[r]) for r in range(N)])
            h = mx_ref.matmul(qu[q], came)
            mark = bits(h, 1 + L, B)
            seen = set(np.delete(bits(g[q], 1 + L, B), top[q]).tolist())
            new = []
            for j in np.flatnonzero(e.reshape(-1) >= 0):
                if int(mark[j]) not in seen:
                    seen.add(int(mark[j]))
                    new.append(int(j))
            new = np.array(new, dtype=int)
            new = new[falling(h[0][new])][:K]
            if len(new): held[q] = put(held[q], np.sort(top[q])[:len(new)], pick(came, new))
            y[q, :, P * t:P * t + P] = mx_ref.matmul(w[q][0], held[q])
    for q in range(N): oc[q], osc[q] = emit(held[q])
    return {"y": y, "oc": oc, "osc": osc}

@@ -1,0 +1,560 @@
+from concourse.bass import DstId, RemoteDMATransfer
+from concourse.mybir import dt, AluOpType, AxisListType, ActivationFunctionType
+
+N, P, K, CAPP, R = 8, 128, 16, 8, 3
+A = R * K
+X0 = 16
+X1 = X0 + N * K
+KB = [X1 + N * (A - K) + 2 * N * K * t for t in range(R + 1)]
+LOW = -1e29
+C, S, F, H, U, I = "float8_e4m3fn_x4", "uint8", "float32", "bfloat16", "uint16", "int32"
+
+
+def _sb(n, d):
+    return ("sbuf", [128, n], d)
+
+
+SCRATCH = {
+    "xt": _sb(512, H), "ut": _sb(512, H), "u2t": _sb(1024, H), "kt": _sb(1024, H),
+    "wq": _sb(1024, C), "wp": _sb(1024, S), "xq": _sb(128, C), "xs": _sb(128, S), "uq": _sb(128, C), "us": _sb(128, S),
+    "urq": _sb(128, C), "urs": _sb(128, S), "u2q": _sb(256, C), "u2s": _sb(256, S), "xpq": _sb(128, C), "xps": _sb(128, S),
+    "sq": _sb(64, C), "sp": _sb(64, S), "fq": _sb(32, C), "fp": _sb(32, S),
+    "q1": _sb(KB[1], C), "s1": _sb(KB[1], S), "q2": _sb(KB[2], C), "s2": _sb(KB[2], S), "q3": _sb(KB[3], C), "s3": _sb(KB[3], S),
+    "pq1": _sb(128, C), "ps1": _sb(128, S), "pq2": _sb(128, C), "ps2": _sb(128, S),
+    "hq": _sb(P + A, C), "hs": _sb(P + A, S), "oq": _sb(128, C), "op": _sb(128, S),
+    "da": ("dram", [N, 128, 1], F), "db": ("dram", [N, 128, 1], F),
+    "tab": _sb(KB[3], F), "tabl": _sb(1032, F), "spool": _sb(KB[3], F),
+    "ci": _sb(16, I), "cf": _sb(48, F), "cu": _sb(16, U), "rows": _sb(192, F),
+    "thr": _sb(128, H), "thq": _sb(256, H), "dm": _sb(128, F), "rs16": _sb(128, F), "hm": _sb(40, F), "tm": _sb(66, H),
+    "rs33": _sb(66, H), "rs65": _sb(260, H), "rs48": _sb(144, H), "one": _sb(48, H), "idc": _sb(96, F), "jfr": _sb(64, F),
+    "oc48": _sb(160, F),
+    "xg": _sb(16, F), "sg": _sb(256, H), "fl": _sb(260, H), "fs": _sb(260, H), "ob": _sb(32, H), "orow": _sb(128, H),
+    "ne": _sb(384, H), "nr": _sb(384, H), "so": _sb(8, U), "xm": _sb(32, F), "plb": _sb(8, F), "mrow": _sb(48, F),
+    "mst": _sb(144, F), "md": _sb(96, F), "me2": _sb(96, F), "mu": _sb(8, U), "mc": _sb(48, F), "ml": _sb(48, F),
+    "ax": _sb(16, F), "au": _sb(24, U), "xr": _sb(192, F),
+    "sid": _sb(48, F), "ssc": _sb(48, F), "smk": _sb(48, F), "spl": _sb(48, F),
+    "cid": _sb(144, F), "csc": _sb(128, F), "cmk": _sb(128, F),
+    "bits": _sb(40, F), "hz": _sb(40, F), "ku": _sb(4, U), "eqb": _sb(66, H), "eqm": _sb(66, H), "eqs": _sb(66, F),
+    "sm": _sb(32, F), "pu": _sb(2, U), "c2a": _sb(32, F), "c2": _sb(32, F), "pay": _sb(32, F), "win": _sb(3 * 224, F),
+    "tb": _sb(512, F), "gcf": _sb(12, F), "gu": _sb(8, U), "dd": _sb(6 * 192, F), "vu": _sb(4, U), "ru": _sb(4, U),
+    "ar": _sb(192, F), "dg": _sb(48, F), "dgs": _sb(48, F), "ou": _sb(4, U), "srt": _sb(64, F), "tc": _sb(128, F),
+    "po": _sb(8, U), "pr": _sb(48 * 4, F), "pou": _sb(4, U), "bm": _sb(64, F), "bt": _sb(64, F), "bu": _sb(16, U),
+    "lr": _sb(256, H), "lf": _sb(128, F), "lu": _sb(16, U), "yb": _sb(384, F), "yn": _sb(16, F),
+}
+for _b in range(8):
+    SCRATCH["pb%d" % _b] = ("psum", [128, 512], F)
+SEMAPHORES = ["nv", "na", "nt", "ng", "sent", "in1", "in2", "in3", "hand"] + ["d%d" % i for i in range(24)]
+
+ADD, SUB, MUL, MAX, MIN = AluOpType.add, AluOpType.subtract, AluOpType.mult, AluOpType.max, AluOpType.min
+GE, GT, LE, LT, EQ, NE = AluOpType.is_ge, AluOpType.is_gt, AluOpType.is_le, AluOpType.is_lt, AluOpType.is_equal, AluOpType.not_equal
+AND = AluOpType.bitwise_and
+ACT = ActivationFunctionType
+U8 = dt.uint8
+
+
+def _write(g, T, topo, src, dsts, pairs, lanes, sem):
+    n = len(lanes) // len(pairs)
+    ids = [DstId(rid=topo.addr(c)[0], pnc=topo.addr(c)[1]) for c in dsts]
+    tf = []
+    for i, (a, b) in enumerate(pairs):
+        m = sum(1 << e for e in lanes[i * n:i * n + n])
+        tf.append(RemoteDMATransfer(dst_ids=ids, dma_engine_mask=m, remote_sem=T.sem[sem], srcs=[a], dsts=[b] * len(ids)))
+    g.remote_dma_fused(tf, local_sem=T.sem.sent)
+    return n * len(pairs)
+
+
+def _lanes(topo, src, dsts):
+    return [e for e in topo.engines(src, dsts[0]) if all(e in topo.engines(src, c) for c in dsts)]
+
+
+def _helpers(T, topo, home):
+    r = T.rank_of(home)
+    peers = [T.cores[(r + d) % N] for d in range(1, N)]
+    near = [c for c in peers if topo.same_plane(topo.chip(home), topo.chip(c))]
+    far = [c for c in peers if c not in near]
+    free = sorted((c for c in topo.cores_of(home) if T.rank_of(c) is None), key=lambda c: topo.die(c) == topo.die(home))
+    hf = [c for c in free if all(topo.may_write(c, d) for d in far)][0]
+    hn = [c for c in free if c != hf and all(topo.may_write(c, d) for d in near)][0]
+    return [(hf, far), (hn, near)]
+
+
+def _hand_on(g, core, T, topo):
+    for home in T.cores:
+        if topo.chip(home) != topo.chip(core):
+            continue
+        for h, dsts in _helpers(T, topo, home):
+            if h == core:
+                r = T.rank_of(home)
+                peers = [c for c in T.cores if c != home]
+                spare = [e for e in topo.engines(home, h) if e not in _lanes(topo, home, peers)]
+                a1 = X1 + (A - K) * r
+                lanes = _lanes(topo, h, dsts)
+                g.wait_ge(T.sem.hand, 2 * len(spare))
+                n = _write(g, T, topo, h, dsts, [(T.fq[:].bitcast(U8), T.q1[:, a1:a1 + 32].bitcast(U8))], lanes, "in3")
+                n += _write(g, T, topo, h, dsts, [(T.fp[:], T.s1[:, a1:a1 + 32])], lanes, "in3")
+                g.wait_ge(T.sem.sent, n)
+
+
+def rank_program(g, core, T, topo):
+    me = T.rank_of(core)
+    if me is None:
+        _hand_on(g, core, T, topo)
+        return
+    eng = {"v": g.vector, "a": g.scalar, "t": g.tensor, "g": g, "s": g.sync}
+    own = {"v": "nv", "a": "na", "t": "nt", "g": "ng"}
+    total, seen, wrote, readers, ndma = {}, {q: {} for q in eng}, {}, {}, [0]
+
+    def wait(q, tok):
+        if seen[q].get(tok[0], 0) < tok[1] and not (q == "t" and tok[0] == "nt"):
+            eng[q].wait_ge(T.sem[tok[0]], tok[1])
+            seen[q][tok[0]] = tok[1]
+
+    def ahead(q, r, w):
+        need = {}
+        for k in r.split() + w.split():
+            for tok in ([wrote[k]] if k in wrote else []) + (readers.get(k, []) if k in w.split() else []):
+                need[tok[0]] = max(need.get(tok[0], 0), tok[1])
+        for tok in need.items():
+            wait(q, tok)
+
+    def behind(tok, r, w):
+        for k in r.split():
+            readers.setdefault(k, []).append(tok)
+        for k in w.split():
+            wrote[k], readers[k] = tok, []
+
+    def op(q, call, r, w):
+        ahead(q, r, w)
+        s = own[q]
+        total[s] = total.get(s, 0) + 1
+        call(eng[q]).then_inc(T.sem[s], 1)
+        behind((s, total[s]), r, w)
+
+    def dma(q, out, in_, r, w):
+        ahead(q, r, w)
+        s = "d%d" % ndma[0]
+        ndma[0] += 1
+        total[s] = 16
+        eng[q].dma_start(out, in_).then_inc(T.sem[s], 16)
+        behind((s, 16), r, w)
+
+    def ts(out, a, s1, o1, r, w, s2=None, o2=None):
+        if o2 is None:
+            op("v", lambda e: e.tensor_scalar(out, a, s1, None, o1), r, w)
+        else:
+            op("v", lambda e: e.tensor_scalar(out, a, s1, s2, o1, o2), r, w)
+
+    def tt(out, a, b, o, r, w):
+        op("v", lambda e: e.tensor_tensor(out, a, b, o), r, w)
+
+    def cp(out, a, r, w):
+        op("v", lambda e: e.tensor_copy(out, a), r, w)
+
+    def fill(out, v, w):
+        op("v", lambda e: e.memset(out, v), "", w)
+
+    def scan(out, keep, a, r, w):
+        op("v", lambda e: e.tensor_tensor_scan(out, keep, a, 0.0, MUL, ADD), r, w)
+
+    def red(out, a, o, r, w, ab=False):
+        op("v", lambda e: e.tensor_reduce(out, a, AxisListType.X, o, apply_absolute_value=ab), r, w)
+
+    def tr(out, a, r, w):
+        op("v", lambda e: e.transpose(out, a), r, w)
+
+    def act(out, a, f, r, w, bias=0.0, scale=1.0, acc=None):
+        op("a", lambda e: e.activation(out, a, f, bias=bias, scale=scale, accum_out=acc), r, w)
+
+    def acp(out, a, r, w):
+        op("a", lambda e: e.activation(out, a, ACT.Copy), r, w)
+
+    def iota(out, pat, base, cm, w):
+        op("g", lambda e: e.iota(out, pat, base, cm, allow_small_or_imprecise_dtypes=True), "", w)
+
+    def quant(q, s, a, r, w):
+        op("v", lambda e: e.quantize_mx(q, s, a), r, w)
+
+    def mm(out, lq, ls, rq, rs, r, w, start=True, stop=True):
+        op("t", lambda e: e.matmul_mx(out, lq, ls, rq, rs, start, stop), r, w)
+
+    def pick(q, s, wq, ws, off, r, w):
+        cp(q.bitcast(dt.uint32), wq.bitcast(dt.uint32).indirect(off), r, w + "q")
+        acp(s, ws.indirect(off), r, w + "s")
+
+    peers = [T.cores[(me + d) % N] for d in range(1, N)]
+    assert all(topo.may_write(core, c) for c in peers)
+    lanes = _lanes(topo, core, peers)
+    hands = [h for h, _d in _helpers(T, topo, core)]
+    spare = [e for e in _lanes(topo, core, hands) if e not in lanes]
+
+    def send(dsts, pairs, use, sem, r):
+        ahead("g", r, "")
+        total["sent"] = total.get("sent", 0) + _write(g, T, topo, core, dsts, pairs, use, sem)
+
+    for s, calls in (("in1", 2), ("in2", 1), ("in3", 2)):
+        total[s] = calls * len(lanes) * len(peers)
+        wrote[s] = (s, total[s])
+
+    pb = [T["pb%d" % b] for b in range(8)]
+    tab, cf, ci, cu, rows, sm = T.tab, T.cf, T.ci, T.cu, T.rows, T.sm
+    a0, a1 = X0 + K * me, X1 + (A - K) * me
+
+    dma("s", T.xt[:], T.x[:], "", "xt")
+    dma("a", T.ut[:], T.u[:], "", "ut")
+    dma("s", T.wq[:].bitcast(U8), T.wc[:], "", "wq")
+    dma("s", T.wp[:], T.ws[:], "", "wp")
+    op("g", lambda e: e.iota(ci[:, 0:1], [[1, 1]], 0, 1), "", "ci0")
+    iota(tab[:, 0:192], [[1, 192]], 0, 0, "taba")
+    iota(rows[:, 0:128], [[0, 8], [1, 16]], 0, 0, "r16")
+    iota(rows[:, 128:160], [[1, 2], [2, 16]], 0, 0, "rn")
+    iota(rows[:, 160:192], [[128, 2], [1, 16]], 0, 0, "rk")
+    iota(tab[:, 192:KB[3]], [[1, KB[3] - 192]], 192, 0, "tabb")
+    o48 = T.oc48
+    fill(cu[:, 0:8], 0, "zo")
+    fill(T.one[:], 1.0, "one")
+    fill(T.hm[:], 2.0, "hm")
+    fill(T.rs48[:], 1.0, "rs48")
+    fill(o48[:], 0.0, "o48")
+    for i, m in enumerate((15, 112, 16, 7, 8)):
+        ts(ci[:, i + 1:i + 2], ci[:, 0:1], m, AND, "ci0", "ci%d" % (i + 1))
+    fill(T.hm[:, 0:40:10], 0.0, "hm")
+    fill(T.rs48[:, 0:144:48], 0.0, "rs48")
+    fill(o48[:, 0:16], 1.0, "o48")
+    cp(cf[:, 0:6], ci[:, 0:6], "ci0 ci1 ci2 ci3 ci4 ci5", "cf")
+    fill(o48[:, 64:96], 1.0, "o48")
+    fill(T.plb[:], 0.0, "plb")
+    pcol, zcol = cf[:, 0:1], cf[:, 1:2]
+    ts(T.thr[:], tab[:, 0:128], pcol, LT, "taba cf", "thr", 0.5, SUB)
+    ts(cf[:, 8:12], tab[:, 0:64:16], zcol, ADD, "taba cf", "jc")
+    jc = [cf[:, 8 + a:9 + a] for a in range(4)]
+    ts(cf[:, 6:7], cf[:, 4:5], 16.0, MUL, "cf", "c6")
+    ts(o48[:, 96:112], tab[:, 0:16], float(a0), ADD, "taba o48", "o48a")
+    ts(cf[:, 7:8], cf[:, 5:6], 0.125, MUL, "cf c6", "c7", cf[:, 6:7], ADD)
+    ts(o48[:, 112:144], tab[:, 0:32], float(a1), ADD, "taba o48", "o48b")
+    ts(cu[:, 8:16], tab[:, 0:16:2], cf[:, 7:8], ADD, "taba c7", "xpo")
+
+    quant(T.uq[:], T.us[:], T.ut[:], "ut", "uq")
+    quant(T.xq[:], T.xs[:], T.xt[:], "xt", "xq")
+    pick(T.urq[:], T.urs[:], T.uq[:], T.us[:], cu[:, 0:8], "uq zo", "ur")
+    mm(pb[0][:, 0:128], T.xq[:], T.xs[:], T.uq[:], T.us[:], "xq uq", "p0")
+    mm(pb[1][:, 0:128], T.urq[:], T.urs[:], T.xq[:], T.xs[:], "xq urq urs", "p1")
+    cp(T.xg[:, 0:1], pb[0][:, 0:1], "", "p0 xg")
+    cp(T.xpq[:].bitcast(dt.uint32), T.xq[:].bitcast(dt.uint32).indirect(cu[:, 8:16]), "xq xpo", "xpq")
+    act(T.sg[:, 0:128], pb[1][:, 0:128], ACT.Sign, "xg", "p1 sg0 sg1", bias=T.xg[:, 0:1], scale=-1.0)
+    acp(T.xps[:], T.xs[:].indirect(cu[:, 8:16]), "xq xpo", "xps")
+    mm(pb[2][:, 0:128], T.xpq[:], T.xps[:], T.uq[:], T.us[:], "xpq xps uq", "p2")
+    tt(T.fl[:, 0:128], T.sg[:, 0:128], T.thr[:], LT, "sg0 sg1 thr", "fl0 fl1 fl2")
+    red(T.xg[:, 1:2], T.fl[:, 0:128], ADD, "fl0", "xo")
+    ts(T.ob[:], T.one[:, 0:32], T.xg[:, 1:2], MUL, "xo one", "ob")
+    for a in range(4):
+        tr(T.orow[0:32, 32 * a:32 * a + 32], T.ob[32 * a:32 * a + 32, :], "ob", "or%d" % a)
+    orow = "or0 or1 or2 or3"
+
+    def miss(c):
+        ts(T.ne[0:32, 128 * c:128 * c + 128], T.orow[0:32, :], cf[0:32, 8 + c:9 + c], NE, orow + " jc", "ne%d" % c)
+
+    def after(c):
+        v = slice(128 * c, 128 * c + 128)
+        scan(T.nr[0:32, v], T.ne[0:32, v], T.ne[0:32, v], "ne%d" % c, "nr%d" % c)
+
+    miss(0)
+    miss(1)
+    after(0)
+    miss(2)
+    for b in range(4):
+        ts(T.so[32 * b:32 * b + 32, 0:1], T.nr[0:32, 127:128], -1.0, MUL, "nr0", "so%d" % b, 127.0, ADD)
+    so = "so0 so1 so2 so3"
+    pick(T.sq[:, 0:16], T.sp[:, 0:16], T.xq[:], T.xs[:], T.so[:, 0:1], "xq " + so, "sa")
+    send(peers, [(T.sq[:, 0:16].bitcast(U8), T.q1[:, a0:a0 + 16].bitcast(U8))], lanes, "in1", "saq")
+    send(peers, [(T.sp[:, 0:16], T.s1[:, a0:a0 + 16])], lanes, "in1", "sas")
+
+    after(1)
+    after(2)
+    ts(T.xm[:, 0:10], pb[2][:, 4:14], 0.0, GT, "", "p2 xm0")
+    for b in range(4):
+        ts(T.so[32 * b:32 * b + 32, 2:4], T.nr[0:32, 255:384:128], -1.0, MUL, "nr1 nr2", "sp%d" % b, 127.0, ADD)
+    sp = "sp0 sp1 sp2 sp3"
+    scan(T.xm[:, 16:26], T.hm[:, 20:30], T.xm[:, 0:10], "hm xm0", "xm1")
+    cp(T.mu[:, 0:1], T.so[:, 0:1], so, "mu0")
+    cp(T.mu[:, 1:3], T.so[:, 2:4], sp, "mu1")
+    ts(T.xm[:, 28:29], T.xm[:, 25:26], 1.0, ADD, "xm1", "xm2")
+    dma("s", T.da[me], T.xm[:, 28:29], "xm2", "da")
+    cp(T.mc[:, 0:3], T.mu[:, 0:3], "mu0 mu1", "mc")
+    cp(T.mrow[:], tab[:, 0:128].indirect(T.mu[:, 0:3]), "taba mu0 mu1", "mrow")
+    pick(T.sq[:, 16:48], T.sp[:, 16:48], T.xq[:], T.xs[:], T.so[:, 2:4], "xq " + sp, "sb")
+    send(hands, [(T.sq[:, 16:48].bitcast(U8), T.fq[:].bitcast(U8))], spare, "hand", "sbq")
+    send(hands, [(T.sp[:, 16:48], T.fp[:])], spare, "hand", "sbs")
+    for c in range(3):
+        ts(T.fl[:, 48 * c:48 * c + 48], T.mrow[:], T.mc[:, c:c + 1], LT, "mrow mc", "fl%d" % c)
+    cp(T.plb[:, 7:8], T.so[:, 0:1], so + " plb", "plb3")
+    scan(T.fs[:, 0:144], T.rs48[:], T.fl[:, 0:144], "rs48 fl0 fl1 fl2", "fs")
+    ts(T.dm[:], rows[:, 0:128], zcol, EQ, "r16 cf", "dm")
+    cp(T.mu[:, 4:7], T.fs[:, 47:144:48], "fs", "mu4")
+    ts(T.rs16[:], rows[:, 0:128], 0.0, GT, "r16", "rs16")
+    sl = T.mu[:, 4:7]
+    cp(T.mst[:, 96:144].indirect(sl), o48[:, 0:48], "o48 mu4", "ms2")
+    cp(T.mst[:, 0:48].indirect(sl), T.mrow[:], "mrow mu4", "ms0")
+    cp(T.mst[:, 48:96].indirect(sl), o48[:, 96:144], "o48a o48b mu4", "ms1")
+    scan(T.ml[:], T.one[:], T.mst[:, 96:144], "one ms2", "ml")
+    tt(T.md[:], T.mst[:, 0:96], T.dm[:, 0:96], MUL, "ms0 ms1 dm", "md")
+    ts(T.mc[:], T.ml[:], zcol, LE, "ml cf", "mc")
+    scan(T.me2[:], T.rs16[:, 0:96], T.md[:], "rs16 md", "me2")
+    red(T.plb[:, 3:4], T.mc[:], ADD, "mc plb", "plb2")
+    cp(T.plb[:, 0:3], T.me2[:, 15:48:16], "me2 plb", "plb0")
+    cp(T.plb[:, 4:7], T.me2[:, 63:96:16], "me2 plb", "plb1")
+    dma("s", T.db[me], T.plb[0:16, :], "plb0 plb1 plb2 plb3", "db")
+    send(peers, [(T.da[me], T.da[me]), (T.db[me], T.db[me])], lanes, "in2", "da db")
+    dma("s", T.ax[:, 0:8], T.da[:], "da in2", "axa")
+    dma("s", T.ax[:, 8:16], T.db[:], "db in2", "axb")
+
+    pick(T.q1[:, a0:a0 + 16], T.s1[:, a0:a0 + 16], T.xq[:], T.xs[:], T.so[:, 0:1], "xq " + so, "oa")
+    pick(T.q1[:, a1:a1 + 32], T.s1[:, a1:a1 + 32], T.xq[:], T.xs[:], T.so[:, 2:4], "xq " + sp, "ob1")
+    fill(T.u2t[:], 0.0, "u2")
+    ts(cf[:, 12:15], tab[:, 0:3], zcol, EQ, "taba cf", "lane")
+    act(T.tabl[:], tab[:, 0:1032], ACT.Identity, "taba tabb lane", "tabl", scale=cf[:, 12:13])
+    for h in range(2):
+        for i in range(3):
+            j = 128 * h + 10 * h + 9 - i
+            cp(T.u2t[:, 4 * j:4 * j + 4], T.ut[:, 4 + 4 * i:8 + 4 * i], "ut u2", "u2%d%d" % (h, i))
+        j = 128 * h + 20 + 10 * h
+        cp(T.u2t[:, 4 * j:4 * j + 40], T.ut[:, 16:56], "ut u2", "u2%d3" % h)
+    quant(T.u2q[:], T.u2s[:], T.u2t[:], "u200 u201 u202 u203 u210 u211 u212 u213", "u2q")
+    w00 = (T.wq[:, 0:128], T.wp[:, 0:128])
+    mm(pb[3][:, 0:128], w00[0], w00[1], T.xq[:], T.xs[:], "wq wp xq", "p3")
+    acp(T.yb[:, 0:128], pb[3][:, 0:128], "", "p3 yb0")
+    acp(T.lf[:], tab[:, 0:128], "taba", "lf")
+    ts(cf[:, 16:17], cf[:, 3:4], 0.5, MUL, "cf", "e8")
+    ts(cf[:, 17:18], cf[:, 3:4], 0.5, MUL, "cf", "e16", float(CAPP), ADD)
+    ts(cf[:, 18:20], cf[:, 8:10], 192.0, ADD, "jc", "dump")
+    ts(cf[:, 20:22], tab[:, 0:2], zcol, ADD, "taba cf", "nn", zcol, ADD)
+    fill(T.tm[:], 1.0, "tm")
+    fill(T.rs33[:], 1.0, "rs33")
+    for h in range(2):
+        ts(T.tm[:, 33 * h + 1:33 * h + 33], rows[:, 128:160], cf[:, 20 + h:21 + h], LT, "rn nn tm", "tm%d" % h)
+    fill(T.rs33[:, 0:66:33], 0.0, "rs33")
+    for t in range(R):
+        ts(cf[:, 32 + t:33 + t], cf[:, 2:3], float(KB[t]), ADD, "cf", "kb%d" % t)
+    ts(T.lu[:, 8:10], tab[:, 0:129:128], pcol, ADD, "taba cf", "ko")
+    for t in range(R):
+        ts(T.idc[:, 32 * t:32 * t + 32], rows[:, 160:192], cf[:, 32 + t:33 + t], ADD, "rk lane kb%d" % t, "idc%d" % t, cf[:, 13:14], MUL)
+    fill(T.win[:], 0.0, "win0 win1 win2")
+    ts(cf[:, 24:28:2], cf[:, 8:12:2], 1.0 / 256, MUL, "jc", "jc1a")
+    ts(cf[:, 25:28:2], cf[:, 9:12:2], 0.5, ADD, "jc", "jc1b", 1.0 / 128, MUL)
+    ts(sm[:, 24:28:2], cf[:, 8:12:2], 1.0, ADD, "jc", "hi0 hi2", 1.0 / 256, MUL)
+    ts(T.jfr[:], tab[:, 1:65], 1.0 / 128, MUL, "taba", "jfr")
+    fill(T.rs65[:], 1.0, "rs65")
+    fill(T.spool[:, 0:16], LOW, "spl0")
+    fill(T.rs65[:, 0:260:65], 0.0, "rs65")
+    ts(cf[:, 28:32], cf[:, 8:12], 64.0, ADD, "jc", "j64")
+    for a in range(4):
+        ts(T.thq[:, 64 * a:64 * a + 64], tab[:, 0:64], jc[a], LT, "taba jc", "thq%d" % a, 0.5, SUB)
+    quant(T.hq[:, 0:128], T.hs[:, 0:128], T.xt[:], "xt", "hx")
+
+    pq, ps = [T.q1, T.q2, T.q3], [T.s1, T.s2, T.s3]
+    blk, half = 32 * (me // 2), 16 * (me % 2)
+    tabs = "taba tabb"
+    wrote["pc0q"], wrote["pc0s"] = wrote["ob1q"], wrote["ob1s"]
+
+    def pool(t):
+        return "in1 in3 oaq oas pc%dq pc%ds k%d0 k%d1" % (t, t, t, t)
+
+    def spread(src, lo, hi, r):
+        for b in range(4):
+            tr(T.bt[32 * b:32 * b + 32, lo:hi], src[blk:blk + 32, lo:hi], r, "bt%d" % b)
+
+    def new_columns(t):
+        v = slice(P + K * t, P + K * t + K)
+        pick(T.hq[:, v], T.hs[:, v], pq[t][:], ps[t][:], T.bu[:, 4 * t:4 * t + 1], pool(t) + " bn%d" % t, "h%d" % t)
+
+    def new_y(t):
+        v = slice(K * t + K, P + K * t + K)
+        mm(pb[3][:, 0:128], w00[0], w00[1], T.hq[:, v], T.hs[:, v], "wq wp hx h0q h0s h1q h1s h2q h2s", "p3")
+
+    def put_y(t, q):
+        v = slice(128 * t, 128 * t + 128)
+        cp(T.yb[:, v].indirect(T.bu[:, 4 * t + 2:4 * t + 3]), T.yn[:], "yn bo%d" % t, "yb%d" % t)
+        dma(q, T.y[:, v], T.yb[:, v], "yb%d" % t, "")
+
+    def relist(t):
+        cp(T.lf[:].indirect(T.bu[:, 4 * t + 2:4 * t + 3]), tab[:, P + K * t:P + K * t + K], "taba bo%d" % t, "lf")
+
+    def slots(t, pos, pk):
+        if t == 0:
+            cp(T.au[:, 0:16], T.ax[:], "axa axb", "au")
+            cp(T.au[:, 16:20:2], T.ax[:, 11:16:4], "axb", pk)
+            acp(T.xr[:, 0:128], tab[:, 0:1032].indirect(T.au[:, 0:8]), tabs + " au", "xr")
+            acp(T.smk[:], T.xr[:, 0:128].indirect(T.au[:, 8:11]), "xr au", "smk")
+        else:
+            tt(T.pr[:, 144:192], o48[:, 48:96].indirect(T.ou[:, 0:3]), T.smk[:], MUL, "o48 ou smk", "pr3")
+            acp(T.csc[:, 0:16], T.ssc[:].indirect(pos), "ssc " + pk, "csc")
+
+    def kept(t, pos, pk):
+        if t == 0:
+            acp(T.sid[:], tab[:, 0:KB[0]].indirect(T.au[:, 12:15]), tabs + " au", "sid")
+            acp(T.spl[:], tab[:, 0:128].indirect(T.au[:, 8:11]), tabs + " au", "spl")
+        acp(T.cid[:, 16:32], T.sid[:].indirect(pos), "sid " + pk, "cid")
+        acp(T.cmk[:, 0:16], T.smk[:].indirect(pos), "smk " + pk, "cmk")
+        for d in range(2):
+            acp(T.bm[:, 32 + 16 * d:48 + 16 * d], T.spl[:].indirect(pos), "spl " + pk, "bm%d" % (2 + d))
+
+    poss = [T.au[:, 16:17], T.pou[:, 0:1], T.pou[:, 2:3]]
+    bts = "bt0 bt1 bt2 bt3"
+    for t in range(R):
+        kb, pos, pk = KB[t], poss[t], "pos%d" % t
+        if t == 0:
+            vq, vs, vr = T.q1[:, X0:X1], T.s1[:, X0:X1], "in1 oaq oas"
+        else:
+            vq, vs, vr = T["pq%d" % t][:], T["ps%d" % t][:], "v%dq v%ds" % (t, t)
+        for i in range(8):
+            mm(pb[i][:, 0:128], T.wq[:, 128 * i:128 * i + 128], T.wp[:, 128 * i:128 * i + 128], vq, vs, "wq wp " + vr, "p%d" % i)
+        if t > 0:
+            cp(T.pr[:, 0:48], o48[:, 0:48].indirect(T.ou[:, 0:3]), "o48 ou", "pr0")
+            cp(T.cmk[:].indirect(T.ru[:]), T.ar[:, 128:192], "ru ar2", "cmk")
+            scan(T.pr[:, 48:96], T.one[:], T.pr[:, 0:48], "one pr0", "pr1")
+            cp(T.smk[:].indirect(poss[t - 1]), T.cmk[:, 0:16], "cmk pos%d" % (t - 1), "smk")
+        for m in range(2):
+            for b in range(4):
+                i = 4 * m + b
+                out = T.kt[:, 512 * m + b:512 * m + 512:4]
+                if b == 3:
+                    ts(out, pb[i][:, 0:128], 0.0, MAX, "", "p%d kt%d" % (i, i), 0.05, MUL)
+                else:
+                    act(out, pb[i][:, 0:128], ACT.Relu, "", "p%d kt%d" % (i, i), scale=0.05)
+            v = slice(kb + 128 * m, kb + 128 * m + 128)
+            quant(pq[t][:, v], ps[t][:, v], T.kt[:, 512 * m:512 * m + 512], " ".join("kt%d" % (4 * m + b) for b in range(4)), "k%d%d" % (t, m))
+            w = slice(128 * m, 128 * m + 128)
+            mm(pb[0][:, 0:128], pq[t][:, v], ps[t][:, v], T.u2q[:, w], T.u2s[:, w], "u2q k%d%d" % (t, m), "p0", m == 0, m == 1)
+            if t > 0 and m == 0:
+                ts(T.pr[:, 96:144], T.pr[:, 48:96], zcol, LE, "pr1 cf", "pr2")
+                red(T.pr[:, 144:145], T.pr[:, 96:144], ADD, "pr2", "pr3")
+        v = slice(kb, kb + 256)
+        mm(pb[1][:, 0:256], T.urq[:], T.urs[:], pq[t][:, v], ps[t][:, v], "urq urs k%d0 k%d1" % (t, t), "p1")
+        if t > 0:
+            cp(pos, T.pr[:, 144:145], "pr3", pk)
+            spread(T.bm, 0, 64, "bm0 bm1 bm2 bm3")
+        acp(T.spool[:, v], pb[1][:, 0:256], "", "p1 sk%d" % t)
+        ts(T.bits[:], pb[0][:, 0:40], 0.0, GT, "", "p0 bits")
+        if t > 0:
+            cp(T.bu[:, 4 * t - 4:4 * t:2], T.bt[:, half:64:32], bts, "bn%d bo%d" % (t - 1, t - 1))
+        scan(T.hz[:], T.hm[:], T.bits[:], "hm bits", "hz")
+        ts(T.ku[:], T.hz[:, 9:40:10], 1.0, ADD, "hz", "ku")
+        act(T.eqb[:, 0:66:33], T.hz[:, 9:20:10], ACT.Identity, "hz e8", "eq2", bias=cf[:, 16:17], scale=16.0)
+        act(T.c2a[:], T.spool[:, v].indirect(T.lu[:, 8:10]), ACT.Identity, "sk%d ko lane" % t, "c2a", scale=cf[:, 14:15])
+        act(sm[:, 0:2], T.hz[:, 9:20:10], ACT.Identity, "hz e16", "lim", bias=cf[:, 17:18], scale=16.0)
+        for h in range(2):
+            ts(T.eqb[:, 33 * h + 1:33 * h + 33], tab[:, 0:16].indirect(T.ku[:, 0:2]), 1.0, SUB, "taba ku hz", "eq%d" % h, T.hz[:, 9 + 10 * h:10 + 10 * h], EQ)
+        tt(T.eqm[:], T.eqb[:], T.tm[:], MUL, "eq0 eq1 eq2 tm0 tm1", "eqm")
+        tt(T.c2[:], T.c2a[:], T.idc[:, 32 * t:32 * t + 32], ADD, "c2a idc%d" % t, "c2")
+        scan(T.eqs[:], T.rs33[:], T.eqm[:], "rs33 eqm", "eqs")
+        tt(T.pay[:], T.tabl[:].indirect(T.ku[:, 2:4]), T.c2[:], ADD, "tabl ku c2", "pay")
+        tt(sm[:, 2:4], T.eqs[:, 32:66:33], sm[:, 0:2], GE, "eqs lim", "over")
+        if t > 0:
+            new_columns(t - 1)
+            new_y(t - 1)
+        for h in range(2):
+            ts(T.pu[:, h:h + 1], sm[:, 2 + h:3 + h], cf[:, 18 + h:19 + h], MUL, "over dump eqs", "pu%d" % h, T.eqs[:, 32 + 33 * h:33 + 33 * h], MAX)
+        if t > 0:
+            slots(t, pos, pk)
+            kept(t, pos, pk)
+            acp(T.yn[:], pb[3][:, 112:128], "", "p3 yn")
+        win = T.win[:, 224 * t:224 * t + 224]
+        cp(win.indirect(T.pu[:]), T.pay[:], "pu0 pu1 pay", "win%d" % t)
+        if t > 0:
+            cp(T.xr[:, 0:128].indirect(T.au[:, 8:11]), T.pr[:, 144:192], "pr3 au", "xr")
+        for a in range(4):
+            tr(T.tb[0:32, a:512:4], T.win[32 * a:32 * a + 32, 224 * t:224 * t + 128], "win%d" % t, "tb%d" % a)
+            if t == 0 and a == 1:
+                slots(t, pos, pk)
+        for b in range(4):
+            tt(T.gcf[32 * b:32 * b + 32, :], T.tb[0:32, 128 * b:128 * b + 12], T.tb[0:32, 128 * b + 64:128 * b + 76], ADD, "tb0 tb1 tb2 tb3", "gc%d" % b)
+        gc = "gc0 gc1 gc2 gc3"
+        cp(T.gu[:], T.gcf[:, 0:8], gc, "gu")
+        tt(sm[:, 4:8], T.gcf[:, 0:4], cf[:, 24:28], ADD, gc + " jc1a jc1b", "mid")
+        if t == 0:
+            cp(T.xr[:, 0:128].indirect(T.au[:, 18:19]), o48[:, 144:160], "o48 " + pk, "xr")
+        tt(T.xr[:, 128:192], tab[:, 0:1032].indirect(T.gu[:, 0:4]), T.jfr[:], ADD, tabs + " gu jfr", "xa")
+        if t == 0:
+            mm(pb[2][:, 0:384], T.urq[:], T.urs[:], T.q1[:, X0:kb], T.s1[:, X0:kb], "urq urs in1 in3 oaq oas ob1q ob1s", "p2")
+        for a in (3, 1):
+            n = 144 + 16 * a
+            act(T.dd[:, 192 * a:192 * a + n], T.xr[:, 0:n], ACT.Sign, "xr xa " + gc, "dd%d lo%d" % (a, a), bias=T.gcf[:, a:a + 1], scale=-1.0, acc=sm[:, 8 + a:9 + a])
+            act(T.dd[:, 672 + 96 * a:672 + 96 * a + n], T.xr[:, 0:n], ACT.Sign, "xr xa mid", "de%d hi%d" % (a, a), bias=sm[:, 4 + a:5 + a], scale=-1.0, acc=sm[:, 24 + a:25 + a])
+        for a in (2, 0):
+            ts(T.dd[:, 192 * a:192 * a + 144 + 16 * a], T.xr[:, 0:144 + 16 * a], sm[:, 4 + a:5 + a], SUB, "xr xa mid", "dd%d" % a)
+        for a in (2, 0):
+            red(sm[:, 8 + a:9 + a], T.dd[:, 192 * a:192 * a + 144 + 16 * a], MIN, "dd%d" % a, "lo%d" % a, ab=True)
+        for a in (2, 3, 0, 1):
+            ts(T.vu[:, a:a + 1], sm[:, 8 + a:9 + a], sm[:, 24 + a:25 + a], GE, "lo%d hi%d " % (a, a) + gc, "vu%d" % a, T.gcf[:, 4 + a:5 + a], MUL)
+        if t == 0:
+            acp(T.spool[:, X0:kb], pb[2][:, 0:384], "", "p2 spx")
+        ends = "lo0 lo1 lo2 lo3 hi0 hi1 hi2 hi3"
+        tt(sm[:, 12:16], sm[:, 8:12], sm[:, 24:28], LT, ends, "fall")
+        acp(T.srt[:], T.spool[:, 0:kb + 256].indirect(T.vu[:]), "spl0 spx sk0 sk1 sk2 vu0 vu1 vu2 vu3", "srt srt0")
+        tt(T.rs65[:, 64:260:65], sm[:, 8:12], sm[:, 24:28], GE, ends + " rs65", "stay")
+        tt(T.fl[:, 64:260:65], sm[:, 12:16], cf[:, 28:32], MUL, "fall j64", "fl0 fl1 fl2 fl3 flb")
+        for a in range(4):
+            act(T.sg[:, 64 * a:64 * a + 64], T.srt[:], ACT.Sign, "srt " + gc, "sg%d" % a, bias=T.gcf[:, 8 + a:9 + a], scale=-1.0)
+        if t > 0:
+            put_y(t - 1, "s")
+            relist(t - 1)
+        if t == R - 1:
+            spread(T.bm, 32, 64, "bm2 bm3")
+            acp(T.yb[:, 128 * t:128 * t + 128], T.yb[:, 128 * t - 128:128 * t], "yb%d" % (t - 1), "yb%d" % t)
+        for a in range(4):
+            tt(T.fl[:, 65 * a:65 * a + 64], T.sg[:, 64 * a:64 * a + 64], T.thq[:, 64 * a:64 * a + 64], LT, "sg%d thq%d flb" % (a, a), "fl%d" % a)
+        if t == 0:
+            acp(T.ssc[:], T.spool[:, 0:kb].indirect(T.au[:, 12:15]), "spl0 spx au", "ssc")
+            acp(T.csc[:, 0:16], T.ssc[:].indirect(pos), "ssc " + pk, "csc")
+            kept(t, pos, pk)
+        acp(T.ar[:, 64:128], tab[:].indirect(T.gu[:, 4:8]), tabs + " gu", "ar1")
+        if t == R - 1:
+            cp(T.bu[:, 4 * t + 2:4 * t + 3], T.bt[:, 32 + half:33 + half], bts, "bo%d" % t)
+        scan(T.fs[:], T.rs65[:], T.fl[:], "rs65 stay fl0 fl1 fl2 fl3 flb", "fs")
+        if t == R - 1:
+            relist(t)
+        cp(T.ru[:], T.fs[:, 64:260:65], "fs", "ru")
+        if t + 1 < R:
+            cp(T.csc[:].indirect(T.ru[:]), T.srt[:], "ru srt", "csc")
+            acp(T.ar[:, 128:192], tab[:, 0:1032].indirect(T.gu[:, 0:4]), tabs + " gu", "ar2")
+            if t > 0:
+                acp(T.yb[:, 128 * t:128 * t + 128], T.yb[:, 128 * t - 128:128 * t], "yb%d" % (t - 1), "yb%d" % t)
+            cp(T.ssc[:].indirect(pos), T.csc[:, 0:16], "csc " + pk, "ssc")
+            tt(T.dg[:], T.ssc[:], T.dm[:, 0:48], MUL, "ssc dm", "dg")
+            scan(T.dgs[:], T.rs16[:, 0:48], T.dg[:], "rs16 dg", "dgs")
+            for c in range(3):
+                act(T.sg[:, 64 * c:64 * c + 48], T.ssc[:], ACT.Sign, "ssc dgs", "sg%d" % c, bias=T.dgs[:, 16 * c + 15:16 * c + 16], scale=-1.0)
+            cp(T.cid[:, 16:144].indirect(T.ru[:]), T.ar[:, 64:128], "ru ar1", "cid")
+            for c in range(3):
+                tt(T.ne[:, 48 * c:48 * c + 48], T.sg[:, 64 * c:64 * c + 48], T.thq[:, 64 * c:64 * c + 48], LT, "sg%d thq%d" % (c, c), "ne0 ne1 ne2 nf%d" % c if c == 0 else "nf%d" % c)
+            for d in range(2):
+                acp(T.bm[:, 16 * d:16 * d + 16], T.cid[:, 16:32], "cid", "bm%d" % d)
+            cp(T.sid[:].indirect(pos), T.cid[:, 16:32], "cid " + pk, "sid")
+            scan(T.nr[:, 0:144], T.rs48[:], T.ne[:, 0:144], "rs48 nf0 nf1 nf2", "nr0 nr1 nr2")
+            cp(T.ou[:, 0:3], T.nr[:, 47:144:48], "nr0", "ou")
+            cp(T.srt[:, 16:64].indirect(T.ou[:, 0:3]), T.sid[:], "ou sid", "srt")
+            cp(T.srt[:, 0:16], T.srt[:, 16:32], "srt", "srt0")
+            for a in range(4):
+                tr(T.tc[0:32, 32 * a:32 * a + 32], T.srt[32 * a:32 * a + 32, 0:32], "srt srt0", "tc%d" % a)
+            for b in range(4):
+                cp(T.po[32 * b:32 * b + 32, :], T.tc[0:32, 0:128:16], "tc0 tc1 tc2 tc3", "po%d" % b)
+            pick(T["pq%d" % (t + 1)][:], T["ps%d" % (t + 1)][:], pq[t][:], ps[t][:], T.po[:], pool(t) + " po0 po1 po2 po3", "v%d" % (t + 1))
+            dma("s", pq[t + 1][:, X0:KB[t + 1]].bitcast(U8), pq[t][:, X0:KB[t + 1]].bitcast(U8), pool(t), "pc%dq" % (t + 1))
+            dma("s", ps[t + 1][:, X0:KB[t + 1]], ps[t][:, X0:KB[t + 1]], pool(t), "pc%ds" % (t + 1))
+    t = R - 1
+    cp(T.cid[:, 16:144].indirect(T.ru[:]), T.ar[:, 64:128], "ru ar1", "cid")
+    cp(T.cid[:, 0:16], T.cid[:, 16:32], "cid", "cid0")
+    spread(T.cid, 0, 32, "cid cid0")
+    cp(T.bu[:, 4 * t:4 * t + 1], T.bt[:, half:half + 1], bts, "bn%d" % t)
+    new_columns(t)
+    new_y(t)
+    tt(T.lr[:, 0:128], T.lf[:], T.dm[:], MUL, "lf dm", "lr0")
+    acp(T.yn[:], pb[3][:, 112:128], "", "p3 yn")
+    scan(T.lr[:, 128:256], T.rs16[:], T.lr[:, 0:128], "rs16 lr0", "lr1")
+    put_y(t, "s")
+    cp(T.lu[:, 0:8], T.lr[:, 143:256:16], "lr1", "lu")
+    pick(T.oq[:], T.op[:], T.hq[:], T.hs[:], T.lu[:, 0:8], "hx h0q h0s h1q h1s h2q h2s lu", "o")
+    dma("s", T.oc[:], T.oq[:].bitcast(U8), "oq", "")
+    for k in range(4):
+        dma("s" if k == 3 else "a", T.osc[4 * k:4 * k + 4, :], T.op[32 * k:32 * k + 4, :], "os", "")
+    for tok in total.items():
+        wait("g", tok)

@@ -17,33 +17,33 @@ def _sb(n, d):
 SCRATCH = {
     "xt": _sb(512, H), "ut": _sb(512, H), "u2t": _sb(1024, H), "kt": _sb(1024, H),
     "wq": _sb(1024, C), "wp": _sb(1024, S), "xq": _sb(128, C), "xs": _sb(128, S), "uq": _sb(128, C), "us": _sb(128, S),
-    "urq": _sb(128, C), "urs": _sb(128, S), "u2q": _sb(256, C), "u2s": _sb(256, S), "xpq": _sb(128, C), "xps": _sb(128, S),
-    "sq": _sb(64, C), "sp": _sb(64, S), "fq": _sb(32, C), "fp": _sb(32, S),
+    "urq": _sb(128, C), "urs": _sb(128, S), "u2q": _sb(256, C), "u2s": _sb(256, S),
+    "sq": _sb(64, C), "sp": _sb(64, S), "fq": _sb(32, C), "fp": _sb(32, S), "fd": ("dram", [128, 1], F),
     "q1": _sb(KB[1], C), "s1": _sb(KB[1], S), "q2": _sb(KB[2], C), "s2": _sb(KB[2], S), "q3": _sb(KB[3], C), "s3": _sb(KB[3], S),
     "pq1": _sb(128, C), "ps1": _sb(128, S), "pq2": _sb(128, C), "ps2": _sb(128, S),
     "hq": _sb(P + A, C), "hs": _sb(P + A, S), "oq": _sb(128, C), "op": _sb(128, S),
-    "da": ("dram", [N, 128, 1], F), "db": ("dram", [N, 128, 1], F),
+    "da": ("dram", [N, 128, 1], F), "lx": _sb(64, U), "lxf": _sb(80, F),
     "tab": _sb(KB[3], F), "tabl": _sb(1032, F), "spool": _sb(KB[3], F),
-    "ci": _sb(16, I), "cf": _sb(48, F), "cu": _sb(16, U), "rows": _sb(192, F),
+    "ci": _sb(16, I), "cf": _sb(48, F), "cu": _sb(24, U), "rows": _sb(320, F),
     "thr": _sb(128, H), "thq": _sb(256, H), "dm": _sb(128, F), "rs16": _sb(128, F), "hm": _sb(40, F), "tm": _sb(66, H),
     "rs33": _sb(66, H), "rs65": _sb(260, H), "rs48": _sb(144, H), "one": _sb(48, H), "idc": _sb(96, F), "jfr": _sb(64, F),
     "oc48": _sb(160, F),
     "xg": _sb(16, F), "sg": _sb(256, H), "fl": _sb(260, H), "fs": _sb(260, H), "ob": _sb(32, H), "orow": _sb(128, H),
-    "ne": _sb(384, H), "nr": _sb(384, H), "so": _sb(8, U), "xm": _sb(32, F), "plb": _sb(8, F), "mrow": _sb(48, F),
-    "mst": _sb(144, F), "md": _sb(96, F), "me2": _sb(96, F), "mu": _sb(8, U), "mc": _sb(48, F), "ml": _sb(48, F),
-    "ax": _sb(16, F), "au": _sb(24, U), "xr": _sb(192, F),
-    "sid": _sb(48, F), "ssc": _sb(48, F), "smk": _sb(48, F), "spl": _sb(48, F),
+    "ne": _sb(384, H), "nr": _sb(384, H), "so": _sb(8, U), "xm": _sb(32, F), "plb": _sb(8, F), "mrow": _sb(96, F),
+    "mst": _sb(208, F), "md": _sb(112, F), "me2": _sb(112, F), "mu": _sb(8, U), "mc": _sb(48, F), "ml": _sb(48, F),
+    "ax": _sb(24, F), "au": _sb(24, U), "xr": _sb(192, F),
+    "sid": _sb(48, F), "ssc": _sb(48, F), "smk": _sb(48, F),
     "cid": _sb(144, F), "csc": _sb(128, F), "cmk": _sb(128, F),
     "bits": _sb(40, F), "hz": _sb(40, F), "ku": _sb(4, U), "eqb": _sb(66, H), "eqm": _sb(66, H), "eqs": _sb(66, F),
     "sm": _sb(32, F), "pu": _sb(2, U), "c2a": _sb(32, F), "c2": _sb(32, F), "pay": _sb(32, F), "win": _sb(3 * 224, F),
     "tb": _sb(512, F), "gcf": _sb(12, F), "gu": _sb(8, U), "dd": _sb(6 * 192, F), "vu": _sb(4, U), "ru": _sb(4, U),
     "ar": _sb(192, F), "dg": _sb(48, F), "dgs": _sb(48, F), "ou": _sb(4, U), "srt": _sb(64, F), "tc": _sb(128, F),
-    "po": _sb(8, U), "pr": _sb(48 * 4, F), "pou": _sb(4, U), "bm": _sb(64, F), "bt": _sb(64, F), "bu": _sb(16, U),
+    "po": _sb(8, U), "pr": _sb(48 * 4, F), "pou": _sb(4, U), "bm": _sb(16 + 256, F), "bt": _sb(48, F), "bu": _sb(16, U),
     "lr": _sb(256, H), "lf": _sb(128, F), "lu": _sb(16, U), "yb": _sb(384, F), "yn": _sb(16, F),
 }
 for _b in range(8):
     SCRATCH["pb%d" % _b] = ("psum", [128, 512], F)
-SEMAPHORES = ["nv", "na", "nt", "ng", "sent", "in1", "in2", "in3", "hand"] + ["d%d" % i for i in range(24)]
+SEMAPHORES = ["nv", "na", "nt", "ng", "sent", "in1", "in2", "in3", "in4", "hand", "hand2"] + ["d%d" % i for i in range(24)]
 
 ADD, SUB, MUL, MAX, MIN = AluOpType.add, AluOpType.subtract, AluOpType.mult, AluOpType.max, AluOpType.min
 GE, GT, LE, LT, EQ, NE = AluOpType.is_ge, AluOpType.is_gt, AluOpType.is_le, AluOpType.is_lt, AluOpType.is_equal, AluOpType.not_equal
@@ -72,26 +72,33 @@ def _helpers(T, topo, home):
     peers = [T.cores[(r + d) % N] for d in range(1, N)]
     near = [c for c in peers if topo.same_plane(topo.chip(home), topo.chip(c))]
     far = [c for c in peers if c not in near]
-    free = sorted((c for c in topo.cores_of(home) if T.rank_of(c) is None), key=lambda c: topo.die(c) == topo.die(home))
-    hf = [c for c in free if all(topo.may_write(c, d) for d in far)][0]
-    hn = [c for c in free if c != hf and all(topo.may_write(c, d) for d in near)][0]
-    return [(hf, far), (hn, near)]
+    free = sorted((c for c in topo.cores_of(home) if T.rank_of(c) is None), key=lambda c: topo.die(c) != topo.die(home))
+    able = [c for c in free if all(topo.may_write(c, d) for d in far)]
+    rest = [c for c in free if c not in able and all(topo.may_write(c, d) for d in near)]
+    return [(able[0], far), (rest[0], near)], [(able[-1], far), (rest[-1], near)]
 
 
 def _hand_on(g, core, T, topo):
     for home in T.cores:
         if topo.chip(home) != topo.chip(core):
             continue
-        for h, dsts in _helpers(T, topo, home):
+        r = T.rank_of(home)
+        a0, a1 = X0 + K * r, X1 + (A - K) * r
+        off = _lanes(topo, home, [c for c in T.cores if c != home])
+        spare = [e for e in topo.engines(home, core) if e not in off]
+        first, later = _helpers(T, topo, home)
+        for h, dsts in first + later:
             if h == core:
-                r = T.rank_of(home)
-                peers = [c for c in T.cores if c != home]
-                spare = [e for e in topo.engines(home, h) if e not in _lanes(topo, home, peers)]
-                a1 = X1 + (A - K) * r
                 lanes = _lanes(topo, h, dsts)
-                g.wait_ge(T.sem.hand, 2 * len(spare))
-                n = _write(g, T, topo, h, dsts, [(T.fq[:].bitcast(U8), T.q1[:, a1:a1 + 32].bitcast(U8))], lanes, "in3")
-                n += _write(g, T, topo, h, dsts, [(T.fp[:], T.s1[:, a1:a1 + 32])], lanes, "in3")
+                if (h, dsts) in first:
+                    g.wait_ge(T.sem.hand, len(off))
+                    n = _write(g, T, topo, h, dsts, [(T.fd[:], T.da[r])], lanes, "in2")
+                    g.wait_ge(T.sem.hand2, len(off))
+                    n += _write(g, T, topo, h, dsts, [(T.fp[:, 0:16], T.s1[:, a0:a0 + 16])], lanes, "in1")
+                else:
+                    g.wait_ge(T.sem.hand, 2 * len(spare))
+                    n = _write(g, T, topo, h, dsts, [(T.fq[:].bitcast(U8), T.q1[:, a1:a1 + 32].bitcast(U8))], lanes, "in3")
+                    n += _write(g, T, topo, h, dsts, [(T.fp[:], T.s1[:, a1:a1 + 32])], lanes, "in3")
                 g.wait_ge(T.sem.sent, n)
 
 
@@ -165,6 +172,9 @@ def rank_program(g, core, T, topo):
     def act(out, a, f, r, w, bias=0.0, scale=1.0, acc=None):
         op("a", lambda e: e.activation(out, a, f, bias=bias, scale=scale, accum_out=acc), r, w)
 
+    def lin(out, a, scale, bias, r, w):
+        act(out, a, ACT.Identity, r, w, bias=bias, scale=scale)
+
     def acp(out, a, r, w):
         op("a", lambda e: e.activation(out, a, ACT.Copy), r, w)
 
@@ -184,20 +194,21 @@ def rank_program(g, core, T, topo):
     peers = [T.cores[(me + d) % N] for d in range(1, N)]
     assert all(topo.may_write(core, c) for c in peers)
     lanes = _lanes(topo, core, peers)
-    hands = [h for h, _d in _helpers(T, topo, core)]
+    first, hands = [[h for h, _d in hs] for hs in _helpers(T, topo, core)]
     spare = [e for e in _lanes(topo, core, hands) if e not in lanes]
 
     def send(dsts, pairs, use, sem, r):
         ahead("g", r, "")
         total["sent"] = total.get("sent", 0) + _write(g, T, topo, core, dsts, pairs, use, sem)
 
-    for s, calls in (("in1", 2), ("in2", 1), ("in3", 2)):
-        total[s] = calls * len(lanes) * len(peers)
+    for s, n in (("in1", 2), ("in2", 1), ("in3", 2), ("in4", 1)):
+        total[s] = n * len(lanes) * len(peers)
         wrote[s] = (s, total[s])
 
     pb = [T["pb%d" % b] for b in range(8)]
     tab, cf, ci, cu, rows, sm = T.tab, T.cf, T.ci, T.cu, T.rows, T.sm
     a0, a1 = X0 + K * me, X1 + (A - K) * me
+    tabs = "taba tabb"
 
     dma("s", T.xt[:], T.x[:], "", "xt")
     dma("a", T.ut[:], T.u[:], "", "ut")
@@ -208,6 +219,7 @@ def rank_program(g, core, T, topo):
     iota(rows[:, 0:128], [[0, 8], [1, 16]], 0, 0, "r16")
     iota(rows[:, 128:160], [[1, 2], [2, 16]], 0, 0, "rn")
     iota(rows[:, 160:192], [[128, 2], [1, 16]], 0, 0, "rk")
+    iota(rows[:, 192:320], [[1, 16], [16, 8]], 0, 0, "rx")
     iota(tab[:, 192:KB[3]], [[1, KB[3] - 192]], 192, 0, "tabb")
     o48 = T.oc48
     fill(cu[:, 0:8], 0, "zo")
@@ -215,23 +227,33 @@ def rank_program(g, core, T, topo):
     fill(T.hm[:], 2.0, "hm")
     fill(T.rs48[:], 1.0, "rs48")
     fill(o48[:], 0.0, "o48")
-    for i, m in enumerate((15, 112, 16, 7, 8)):
+    fill(T.tm[:], 1.0, "tm")
+    fill(T.rs33[:], 1.0, "rs33")
+    fill(T.rs65[:], 1.0, "rs65")
+    for i, m in enumerate((15, 112, 16)):
         ts(ci[:, i + 1:i + 2], ci[:, 0:1], m, AND, "ci0", "ci%d" % (i + 1))
     fill(T.hm[:, 0:40:10], 0.0, "hm")
     fill(T.rs48[:, 0:144:48], 0.0, "rs48")
     fill(o48[:, 0:16], 1.0, "o48")
-    cp(cf[:, 0:6], ci[:, 0:6], "ci0 ci1 ci2 ci3 ci4 ci5", "cf")
+    cp(cf[:, 0:4], ci[:, 0:4], "ci0 ci1 ci2 ci3", "cf")
+    fill(T.rs33[:, 0:66:33], 0.0, "rs33")
+    fill(T.rs65[:, 0:260:65], 0.0, "rs65")
     fill(o48[:, 64:96], 1.0, "o48")
-    fill(T.plb[:], 0.0, "plb")
+    fill(T.lxf[:, 64:80], 0.0, "lxp")
     pcol, zcol = cf[:, 0:1], cf[:, 1:2]
     ts(T.thr[:], tab[:, 0:128], pcol, LT, "taba cf", "thr", 0.5, SUB)
     ts(cf[:, 8:12], tab[:, 0:64:16], zcol, ADD, "taba cf", "jc")
     jc = [cf[:, 8 + a:9 + a] for a in range(4)]
-    ts(cf[:, 6:7], cf[:, 4:5], 16.0, MUL, "cf", "c6")
-    ts(o48[:, 96:112], tab[:, 0:16], float(a0), ADD, "taba o48", "o48a")
-    ts(cf[:, 7:8], cf[:, 5:6], 0.125, MUL, "cf c6", "c7", cf[:, 6:7], ADD)
-    ts(o48[:, 112:144], tab[:, 0:32], float(a1), ADD, "taba o48", "o48b")
-    ts(cu[:, 8:16], tab[:, 0:16:2], cf[:, 7:8], ADD, "taba c7", "xpo")
+    ts(cf[:, 12:15], tab[:, 0:3], zcol, EQ, "taba cf", "lane")
+    ts(cf[:, 20:22], tab[:, 0:2], zcol, ADD, "taba cf", "nn", zcol, ADD)
+    lin(o48[:, 96:112], tab[:, 0:16], 1.0, float(a0), "taba o48", "o48a")
+    lin(o48[:, 112:144], tab[:, 0:32], 1.0, float(a1), "taba o48", "o48b")
+    lin(cf[:, 16:17], cf[:, 3:4], 0.5, 0.0, "cf", "e8")
+    lin(cf[:, 17:18], cf[:, 3:4], 0.5, float(CAPP), "cf", "e16")
+    lin(cf[:, 18:20], cf[:, 8:10], 1.0, 192.0, "jc", "dump")
+    lin(cf[:, 32:35], tab[:, 0:3], 2.0 * N * K, cf[:, 2:3], "taba cf", "kb")
+    lin(cf[:, 35:36], cf[:, 13:14], float(KB[0]), 0.0, "lane", "kb0")
+    lin(cf[:, 36:39], cf[:, 32:35], cf[:, 13:14], cf[:, 35:36], "kb kb0 lane", "kbm")
 
     quant(T.uq[:], T.us[:], T.ut[:], "ut", "uq")
     quant(T.xq[:], T.xs[:], T.xt[:], "xt", "xq")
@@ -239,10 +261,16 @@ def rank_program(g, core, T, topo):
     mm(pb[0][:, 0:128], T.xq[:], T.xs[:], T.uq[:], T.us[:], "xq uq", "p0")
     mm(pb[1][:, 0:128], T.urq[:], T.urs[:], T.xq[:], T.xs[:], "xq urq urs", "p1")
     cp(T.xg[:, 0:1], pb[0][:, 0:1], "", "p0 xg")
-    cp(T.xpq[:].bitcast(dt.uint32), T.xq[:].bitcast(dt.uint32).indirect(cu[:, 8:16]), "xq xpo", "xpq")
+    ts(T.xm[:, 0:10], pb[0][:, 4:14], 0.0, GT, "", "p0 xm0")
     act(T.sg[:, 0:128], pb[1][:, 0:128], ACT.Sign, "xg", "p1 sg0 sg1", bias=T.xg[:, 0:1], scale=-1.0)
-    acp(T.xps[:], T.xs[:].indirect(cu[:, 8:16]), "xq xpo", "xps")
-    mm(pb[2][:, 0:128], T.xpq[:], T.xps[:], T.uq[:], T.us[:], "xpq xps uq", "p2")
+    ts(T.tm[:, 1:33], rows[:, 128:160], cf[:, 20:21], LT, "rn nn tm", "tm0")
+    scan(T.xm[:, 16:26], T.hm[:, 20:30], T.xm[:, 0:10], "hm xm0", "xm1")
+    ts(T.tm[:, 34:66], rows[:, 128:160], cf[:, 21:22], LT, "rn nn tm", "tm1")
+    ts(T.xm[:, 28:29], T.xm[:, 25:26], 1.0, ADD, "xm1", "xm2")
+    send(first, [(T.xm[:, 28:29], T.fd[:])], lanes, "hand", "xm2")
+    dma("s", T.da[me], T.xm[:, 28:29], "xm2", "da")
+    for h in range(2):
+        lin(T.u2t[:, 512 * h:512 * h + 512], T.ut[:], 0.0, 0.0, "ut", "u2%d" % h)
     tt(T.fl[:, 0:128], T.sg[:, 0:128], T.thr[:], LT, "sg0 sg1 thr", "fl0 fl1 fl2")
     red(T.xg[:, 1:2], T.fl[:, 0:128], ADD, "fl0", "xo")
     ts(T.ob[:], T.one[:, 0:32], T.xg[:, 1:2], MUL, "xo one", "ob")
@@ -265,102 +293,69 @@ def rank_program(g, core, T, topo):
         ts(T.so[32 * b:32 * b + 32, 0:1], T.nr[0:32, 127:128], -1.0, MUL, "nr0", "so%d" % b, 127.0, ADD)
     so = "so0 so1 so2 so3"
     pick(T.sq[:, 0:16], T.sp[:, 0:16], T.xq[:], T.xs[:], T.so[:, 0:1], "xq " + so, "sa")
+    send(first, [(T.sp[:, 0:16], T.fp[:, 0:16])], lanes, "hand2", "sas")
     send(peers, [(T.sq[:, 0:16].bitcast(U8), T.q1[:, a0:a0 + 16].bitcast(U8))], lanes, "in1", "saq")
-    send(peers, [(T.sp[:, 0:16], T.s1[:, a0:a0 + 16])], lanes, "in1", "sas")
 
     after(1)
     after(2)
-    ts(T.xm[:, 0:10], pb[2][:, 4:14], 0.0, GT, "", "p2 xm0")
+    pick(T.q1[:, a0:a0 + 16], T.s1[:, a0:a0 + 16], T.xq[:], T.xs[:], T.so[:, 0:1], "xq " + so, "oa")
     for b in range(4):
         ts(T.so[32 * b:32 * b + 32, 2:4], T.nr[0:32, 255:384:128], -1.0, MUL, "nr1 nr2", "sp%d" % b, 127.0, ADD)
     sp = "sp0 sp1 sp2 sp3"
-    scan(T.xm[:, 16:26], T.hm[:, 20:30], T.xm[:, 0:10], "hm xm0", "xm1")
     cp(T.mu[:, 0:1], T.so[:, 0:1], so, "mu0")
     cp(T.mu[:, 1:3], T.so[:, 2:4], sp, "mu1")
-    ts(T.xm[:, 28:29], T.xm[:, 25:26], 1.0, ADD, "xm1", "xm2")
-    dma("s", T.da[me], T.xm[:, 28:29], "xm2", "da")
-    cp(T.mc[:, 0:3], T.mu[:, 0:3], "mu0 mu1", "mc")
-    cp(T.mrow[:], tab[:, 0:128].indirect(T.mu[:, 0:3]), "taba mu0 mu1", "mrow")
     pick(T.sq[:, 16:48], T.sp[:, 16:48], T.xq[:], T.xs[:], T.so[:, 2:4], "xq " + sp, "sb")
+    cp(T.mc[:, 0:3], T.mu[:, 0:3], "mu0 mu1", "mc")
+    cp(T.mrow[:, 0:48], tab[:, 0:128].indirect(T.mu[:, 0:3]), "taba mu0 mu1", "mrow")
+    pick(T.q1[:, a1:a1 + 32], T.s1[:, a1:a1 + 32], T.xq[:], T.xs[:], T.so[:, 2:4], "xq " + sp, "ob1")
     send(hands, [(T.sq[:, 16:48].bitcast(U8), T.fq[:].bitcast(U8))], spare, "hand", "sbq")
     send(hands, [(T.sp[:, 16:48], T.fp[:])], spare, "hand", "sbs")
     for c in range(3):
-        ts(T.fl[:, 48 * c:48 * c + 48], T.mrow[:], T.mc[:, c:c + 1], LT, "mrow mc", "fl%d" % c)
-    cp(T.plb[:, 7:8], T.so[:, 0:1], so + " plb", "plb3")
-    scan(T.fs[:, 0:144], T.rs48[:], T.fl[:, 0:144], "rs48 fl0 fl1 fl2", "fs")
-    ts(T.dm[:], rows[:, 0:128], zcol, EQ, "r16 cf", "dm")
-    cp(T.mu[:, 4:7], T.fs[:, 47:144:48], "fs", "mu4")
-    ts(T.rs16[:], rows[:, 0:128], 0.0, GT, "r16", "rs16")
-    sl = T.mu[:, 4:7]
-    cp(T.mst[:, 96:144].indirect(sl), o48[:, 0:48], "o48 mu4", "ms2")
-    cp(T.mst[:, 0:48].indirect(sl), T.mrow[:], "mrow mu4", "ms0")
-    cp(T.mst[:, 48:96].indirect(sl), o48[:, 96:144], "o48a o48b mu4", "ms1")
-    scan(T.ml[:], T.one[:], T.mst[:, 96:144], "one ms2", "ml")
-    tt(T.md[:], T.mst[:, 0:96], T.dm[:, 0:96], MUL, "ms0 ms1 dm", "md")
-    ts(T.mc[:], T.ml[:], zcol, LE, "ml cf", "mc")
-    scan(T.me2[:], T.rs16[:, 0:96], T.md[:], "rs16 md", "me2")
-    red(T.plb[:, 3:4], T.mc[:], ADD, "mc plb", "plb2")
-    cp(T.plb[:, 0:3], T.me2[:, 15:48:16], "me2 plb", "plb0")
-    cp(T.plb[:, 4:7], T.me2[:, 63:96:16], "me2 plb", "plb1")
-    dma("s", T.db[me], T.plb[0:16, :], "plb0 plb1 plb2 plb3", "db")
-    send(peers, [(T.da[me], T.da[me]), (T.db[me], T.db[me])], lanes, "in2", "da db")
-    dma("s", T.ax[:, 0:8], T.da[:], "da in2", "axa")
-    dma("s", T.ax[:, 8:16], T.db[:], "db in2", "axb")
-
-    pick(T.q1[:, a0:a0 + 16], T.s1[:, a0:a0 + 16], T.xq[:], T.xs[:], T.so[:, 0:1], "xq " + so, "oa")
-    pick(T.q1[:, a1:a1 + 32], T.s1[:, a1:a1 + 32], T.xq[:], T.xs[:], T.so[:, 2:4], "xq " + sp, "ob1")
-    fill(T.u2t[:], 0.0, "u2")
-    ts(cf[:, 12:15], tab[:, 0:3], zcol, EQ, "taba cf", "lane")
-    act(T.tabl[:], tab[:, 0:1032], ACT.Identity, "taba tabb lane", "tabl", scale=cf[:, 12:13])
+        ts(T.fl[:, 48 * c:48 * c + 48], T.mrow[:, 0:48], T.mc[:, c:c + 1], LT, "mrow mc", "fl%d" % c)
+    acp(T.mrow[:, 48:96], rows[:, 192:320].indirect(T.mu[:, 0:3]), "rx mu0 mu1", "mrx")
+    acp(T.mst[:, 96:112], rows[:, 192:320].indirect(T.mu[:, 0:1]), "rx mu0 mu1", "ms3")
     for h in range(2):
         for i in range(3):
             j = 128 * h + 10 * h + 9 - i
-            cp(T.u2t[:, 4 * j:4 * j + 4], T.ut[:, 4 + 4 * i:8 + 4 * i], "ut u2", "u2%d%d" % (h, i))
+            acp(T.u2t[:, 4 * j:4 * j + 4], T.ut[:, 4 + 4 * i:8 + 4 * i], "ut u2%d" % h, "u2%d%d" % (h, i))
         j = 128 * h + 20 + 10 * h
-        cp(T.u2t[:, 4 * j:4 * j + 40], T.ut[:, 16:56], "ut u2", "u2%d3" % h)
+        acp(T.u2t[:, 4 * j:4 * j + 40], T.ut[:, 16:56], "ut u2%d" % h, "u2%d3" % h)
+    lin(T.win[:, 0:224], tab[:, 0:224], 0.0, 0.0, tabs, "win0")
+    lin(T.tabl[:], tab[:, 0:1032], cf[:, 12:13], 0.0, tabs + " lane", "tabl")
+    lin(T.idc[:, 0:32], rows[:, 160:192], cf[:, 13:14], cf[:, 36:37], "rk lane kbm", "idc0")
+    ts(T.dm[:], rows[:, 0:128], zcol, EQ, "r16 cf", "dm")
+    scan(T.fs[:, 0:144], T.rs48[:], T.fl[:, 0:144], "rs48 fl0 fl1 fl2", "fs")
+    ts(T.rs16[:], rows[:, 0:128], 0.0, GT, "r16", "rs16")
+    cp(T.mu[:, 4:7], T.fs[:, 47:144:48], "fs", "mu4")
+    sl = T.mu[:, 4:7]
+    cp(T.mst[:, 112:160].indirect(sl), o48[:, 0:48], "o48 mu4", "ms2")
+    cp(T.mst[:, 0:48].indirect(sl), T.mrow[:, 48:96], "mrx mu4", "ms0")
+    cp(T.mst[:, 48:96].indirect(sl), o48[:, 96:144], "o48a o48b mu4", "ms1")
+    scan(T.ml[:], T.one[:], T.mst[:, 112:160], "one ms2", "ml")
+    tt(T.md[:], T.mst[:, 0:112], T.dm[:, 0:112], MUL, "ms0 ms1 ms3 dm", "md")
+    ts(T.mc[:], T.ml[:], zcol, LE, "ml cf", "mc")
+    scan(T.me2[:], T.rs16[:, 0:112], T.md[:], "rs16 md", "me2")
+    red(T.plb[:, 3:4], T.mc[:], ADD, "mc", "plb")
+    cp(T.lx[:, 8 * me:8 * me + 3], T.me2[:, 15:48:16], "me2", "lx0")
+    cp(T.lx[:, 8 * me + 4:8 * me + 8], T.me2[:, 63:112:16], "me2", "lx1")
+    cp(T.lx[:, 8 * me + 3:8 * me + 4], T.plb[:, 3:4], "plb", "lx2")
+    send(peers, [(T.lx[:, 8 * me:8 * me + 8], T.lx[:, 8 * me:8 * me + 8])], lanes, "in4", "lx0 lx1 lx2")
+    dma("s", T.ax[:, 0:8], T.da[:], "da in2", "axa")
     quant(T.u2q[:], T.u2s[:], T.u2t[:], "u200 u201 u202 u203 u210 u211 u212 u213", "u2q")
-    w00 = (T.wq[:, 0:128], T.wp[:, 0:128])
-    mm(pb[3][:, 0:128], w00[0], w00[1], T.xq[:], T.xs[:], "wq wp xq", "p3")
-    acp(T.yb[:, 0:128], pb[3][:, 0:128], "", "p3 yb0")
-    acp(T.lf[:], tab[:, 0:128], "taba", "lf")
-    ts(cf[:, 16:17], cf[:, 3:4], 0.5, MUL, "cf", "e8")
-    ts(cf[:, 17:18], cf[:, 3:4], 0.5, MUL, "cf", "e16", float(CAPP), ADD)
-    ts(cf[:, 18:20], cf[:, 8:10], 192.0, ADD, "jc", "dump")
-    ts(cf[:, 20:22], tab[:, 0:2], zcol, ADD, "taba cf", "nn", zcol, ADD)
-    fill(T.tm[:], 1.0, "tm")
-    fill(T.rs33[:], 1.0, "rs33")
-    for h in range(2):
-        ts(T.tm[:, 33 * h + 1:33 * h + 33], rows[:, 128:160], cf[:, 20 + h:21 + h], LT, "rn nn tm", "tm%d" % h)
-    fill(T.rs33[:, 0:66:33], 0.0, "rs33")
-    for t in range(R):
-        ts(cf[:, 32 + t:33 + t], cf[:, 2:3], float(KB[t]), ADD, "cf", "kb%d" % t)
     ts(T.lu[:, 8:10], tab[:, 0:129:128], pcol, ADD, "taba cf", "ko")
-    for t in range(R):
-        ts(T.idc[:, 32 * t:32 * t + 32], rows[:, 160:192], cf[:, 32 + t:33 + t], ADD, "rk lane kb%d" % t, "idc%d" % t, cf[:, 13:14], MUL)
-    fill(T.win[:], 0.0, "win0 win1 win2")
-    ts(cf[:, 24:28:2], cf[:, 8:12:2], 1.0 / 256, MUL, "jc", "jc1a")
-    ts(cf[:, 25:28:2], cf[:, 9:12:2], 0.5, ADD, "jc", "jc1b", 1.0 / 128, MUL)
-    ts(sm[:, 24:28:2], cf[:, 8:12:2], 1.0, ADD, "jc", "hi0 hi2", 1.0 / 256, MUL)
-    ts(T.jfr[:], tab[:, 1:65], 1.0 / 128, MUL, "taba", "jfr")
-    fill(T.rs65[:], 1.0, "rs65")
-    fill(T.spool[:, 0:16], LOW, "spl0")
-    fill(T.rs65[:, 0:260:65], 0.0, "rs65")
-    ts(cf[:, 28:32], cf[:, 8:12], 64.0, ADD, "jc", "j64")
-    for a in range(4):
-        ts(T.thq[:, 64 * a:64 * a + 64], tab[:, 0:64], jc[a], LT, "taba jc", "thq%d" % a, 0.5, SUB)
-    quant(T.hq[:, 0:128], T.hs[:, 0:128], T.xt[:], "xt", "hx")
+    ts(cu[:, 8:9], cf[:, 2:3], 0.5, MUL, "cf", "lo8", zcol, ADD)
+    ts(cu[:, 16:24], tab[:, 0:8], 0.0, MUL, "taba cf", "z8", zcol, ADD)
+    w00 = (T.wq[:, 0:128], T.wp[:, 0:128])
 
     pq, ps = [T.q1, T.q2, T.q3], [T.s1, T.s2, T.s3]
     blk, half = 32 * (me // 2), 16 * (me % 2)
-    tabs = "taba tabb"
     wrote["pc0q"], wrote["pc0s"] = wrote["ob1q"], wrote["ob1s"]
 
     def pool(t):
         return "in1 in3 oaq oas pc%dq pc%ds k%d0 k%d1" % (t, t, t, t)
 
-    def spread(src, lo, hi, r):
-        for b in range(4):
-            tr(T.bt[32 * b:32 * b + 32, lo:hi], src[blk:blk + 32, lo:hi], r, "bt%d" % b)
+    def spread(t):
+        dma("s", T.bt[:, 32 + 4 * t:34 + 4 * t], T.bm[16 * me:16 * me + 1, 16:272], "bma bmb", "bt%d" % (4 + t))
 
     def new_columns(t):
         v = slice(P + K * t, P + K * t + K)
@@ -378,27 +373,20 @@ def rank_program(g, core, T, topo):
     def relist(t):
         cp(T.lf[:].indirect(T.bu[:, 4 * t + 2:4 * t + 3]), tab[:, P + K * t:P + K * t + K], "taba bo%d" % t, "lf")
 
-    def slots(t, pos, pk):
-        if t == 0:
-            cp(T.au[:, 0:16], T.ax[:], "axa axb", "au")
-            cp(T.au[:, 16:20:2], T.ax[:, 11:16:4], "axb", pk)
-            acp(T.xr[:, 0:128], tab[:, 0:1032].indirect(T.au[:, 0:8]), tabs + " au", "xr")
-            acp(T.smk[:], T.xr[:, 0:128].indirect(T.au[:, 8:11]), "xr au", "smk")
-        else:
-            tt(T.pr[:, 144:192], o48[:, 48:96].indirect(T.ou[:, 0:3]), T.smk[:], MUL, "o48 ou smk", "pr3")
-            acp(T.csc[:, 0:16], T.ssc[:].indirect(pos), "ssc " + pk, "csc")
+    def first_slots(pk):
+        cp(T.au[:, 0:16], T.ax[:, 0:16], "axa axb", "au")
+        cp(T.au[:, 16:20:2], T.ax[:, 11:16:4], "axb", pk)
+        acp(T.xr[:, 0:128], tab[:, 0:1032].indirect(T.au[:, 0:8]), tabs + " au", "xr")
+        acp(T.smk[:], T.xr[:, 0:128].indirect(T.au[:, 8:11]), "xr au", "smk")
 
     def kept(t, pos, pk):
         if t == 0:
             acp(T.sid[:], tab[:, 0:KB[0]].indirect(T.au[:, 12:15]), tabs + " au", "sid")
-            acp(T.spl[:], tab[:, 0:128].indirect(T.au[:, 8:11]), tabs + " au", "spl")
         acp(T.cid[:, 16:32], T.sid[:].indirect(pos), "sid " + pk, "cid")
         acp(T.cmk[:, 0:16], T.smk[:].indirect(pos), "smk " + pk, "cmk")
-        for d in range(2):
-            acp(T.bm[:, 32 + 16 * d:48 + 16 * d], T.spl[:].indirect(pos), "spl " + pk, "bm%d" % (2 + d))
+        acp(T.bm[:, 0:16], T.mst[:, 160:208].indirect(pos), "spl " + pk, "bm0")
 
     poss = [T.au[:, 16:17], T.pou[:, 0:1], T.pou[:, 2:3]]
-    bts = "bt0 bt1 bt2 bt3"
     for t in range(R):
         kb, pos, pk = KB[t], poss[t], "pos%d" % t
         if t == 0:
@@ -407,7 +395,12 @@ def rank_program(g, core, T, topo):
             vq, vs, vr = T["pq%d" % t][:], T["ps%d" % t][:], "v%dq v%ds" % (t, t)
         for i in range(8):
             mm(pb[i][:, 0:128], T.wq[:, 128 * i:128 * i + 128], T.wp[:, 128 * i:128 * i + 128], vq, vs, "wq wp " + vr, "p%d" % i)
-        if t > 0:
+        if t == 0:
+            cp(T.mst[:, 160:208].indirect(sl), T.mrow[:, 0:48], "mrow mu4", "spl")
+            fill(T.spool[:, 0:16], LOW, "spl0")
+            for a in range(2):
+                ts(T.thq[:, 64 * a:64 * a + 64], tab[:, 0:64], jc[a], LT, "taba jc", "thq%d" % a, 0.5, SUB)
+        else:
             cp(T.pr[:, 0:48], o48[:, 0:48].indirect(T.ou[:, 0:3]), "o48 ou", "pr0")
             cp(T.cmk[:].indirect(T.ru[:]), T.ar[:, 128:192], "ru ar2", "cmk")
             scan(T.pr[:, 48:96], T.one[:], T.pr[:, 0:48], "one pr0", "pr1")
@@ -424,6 +417,11 @@ def rank_program(g, core, T, topo):
             quant(pq[t][:, v], ps[t][:, v], T.kt[:, 512 * m:512 * m + 512], " ".join("kt%d" % (4 * m + b) for b in range(4)), "k%d%d" % (t, m))
             w = slice(128 * m, 128 * m + 128)
             mm(pb[0][:, 0:128], pq[t][:, v], ps[t][:, v], T.u2q[:, w], T.u2s[:, w], "u2q k%d%d" % (t, m), "p0", m == 0, m == 1)
+            if t == 0 and m == 0:
+                for a in range(2, 4):
+                    ts(T.thq[:, 64 * a:64 * a + 64], tab[:, 0:64], jc[a], LT, "taba jc", "thq%d" % a, 0.5, SUB)
+            if t == 0 and m == 1:
+                quant(T.hq[:, 0:128], T.hs[:, 0:128], T.xt[:], "xt", "hx")
             if t > 0 and m == 0:
                 ts(T.pr[:, 96:144], T.pr[:, 48:96], zcol, LE, "pr1 cf", "pr2")
                 red(T.pr[:, 144:145], T.pr[:, 96:144], ADD, "pr2", "pr3")
@@ -431,16 +429,19 @@ def rank_program(g, core, T, topo):
         mm(pb[1][:, 0:256], T.urq[:], T.urs[:], pq[t][:, v], ps[t][:, v], "urq urs k%d0 k%d1" % (t, t), "p1")
         if t > 0:
             cp(pos, T.pr[:, 144:145], "pr3", pk)
-            spread(T.bm, 0, 64, "bm0 bm1 bm2 bm3")
+            cp(T.bu[:, 4 * t - 4:4 * t:2], T.bt[:, 28 + 4 * t:30 + 4 * t], "bt%d" % (3 + t), "bn%d bo%d" % (t - 1, t - 1))
+            tt(T.pr[:, 144:192], o48[:, 48:96].indirect(T.ou[:, 0:3]), T.smk[:], MUL, "o48 ou smk", "pr3")
+        else:
+            mm(pb[3][:, 0:128], w00[0], w00[1], T.xq[:], T.xs[:], "wq wp xq", "p3")
         acp(T.spool[:, v], pb[1][:, 0:256], "", "p1 sk%d" % t)
         ts(T.bits[:], pb[0][:, 0:40], 0.0, GT, "", "p0 bits")
         if t > 0:
-            cp(T.bu[:, 4 * t - 4:4 * t:2], T.bt[:, half:64:32], bts, "bn%d bo%d" % (t - 1, t - 1))
+            cp(T.xr[:, 0:128].indirect(T.au[:, 8:11]), T.pr[:, 144:192], "pr3 au", "xr")
         scan(T.hz[:], T.hm[:], T.bits[:], "hm bits", "hz")
         ts(T.ku[:], T.hz[:, 9:40:10], 1.0, ADD, "hz", "ku")
-        act(T.eqb[:, 0:66:33], T.hz[:, 9:20:10], ACT.Identity, "hz e8", "eq2", bias=cf[:, 16:17], scale=16.0)
-        act(T.c2a[:], T.spool[:, v].indirect(T.lu[:, 8:10]), ACT.Identity, "sk%d ko lane" % t, "c2a", scale=cf[:, 14:15])
-        act(sm[:, 0:2], T.hz[:, 9:20:10], ACT.Identity, "hz e16", "lim", bias=cf[:, 17:18], scale=16.0)
+        lin(T.eqb[:, 0:66:33], T.hz[:, 9:20:10], 16.0, cf[:, 16:17], "hz e8", "eq2")
+        lin(T.c2a[:], T.spool[:, v].indirect(T.lu[:, 8:10]), cf[:, 14:15], 0.0, "sk%d ko lane" % t, "c2a")
+        lin(sm[:, 0:2], T.hz[:, 9:20:10], 16.0, cf[:, 17:18], "hz e16", "lim")
         for h in range(2):
             ts(T.eqb[:, 33 * h + 1:33 * h + 33], tab[:, 0:16].indirect(T.ku[:, 0:2]), 1.0, SUB, "taba ku hz", "eq%d" % h, T.hz[:, 9 + 10 * h:10 + 10 * h], EQ)
         tt(T.eqm[:], T.eqb[:], T.tm[:], MUL, "eq0 eq1 eq2 tm0 tm1", "eqm")
@@ -451,20 +452,31 @@ def rank_program(g, core, T, topo):
         if t > 0:
             new_columns(t - 1)
             new_y(t - 1)
+        else:
+            lin(cf[:, 24:28:2], cf[:, 8:12:2], 1.0 / 256, 0.0, "jc", "jc1a")
+            lin(cf[:, 25:28:2], cf[:, 9:12:2], 1.0 / 128, 1.0 / 256, "jc", "jc1b")
+            lin(T.jfr[:], tab[:, 1:65], 1.0 / 128, 0.0, "taba", "jfr")
+            lin(sm[:, 24:28:2], cf[:, 8:12:2], 1.0 / 256, 1.0 / 256, "jc", "hi0 hi2")
+            lin(cf[:, 28:32], cf[:, 8:12], 1.0, 64.0, "jc", "j64")
         for h in range(2):
             ts(T.pu[:, h:h + 1], sm[:, 2 + h:3 + h], cf[:, 18 + h:19 + h], MUL, "over dump eqs", "pu%d" % h, T.eqs[:, 32 + 33 * h:33 + 33 * h], MAX)
         if t > 0:
-            slots(t, pos, pk)
+            acp(T.csc[:, 0:16], T.ssc[:].indirect(pos), "ssc " + pk, "csc")
             kept(t, pos, pk)
             acp(T.yn[:], pb[3][:, 112:128], "", "p3 yn")
+        else:
+            cp(T.lxf[:, 0:64], T.lx[:], "in4 lx0 lx1 lx2", "lxf")
+            acp(T.ax[:, 8:24], T.lxf[:].indirect(cu[:, 8:9]), "lxf lxp lo8", "axb")
+        if t == R - 1:
+            acp(T.bm[:, 17:272:2], T.bm[:, 0:16].indirect(cu[:, 16:24]), "bm0 z8", "bmb")
+            spread(t)
         win = T.win[:, 224 * t:224 * t + 224]
         cp(win.indirect(T.pu[:]), T.pay[:], "pu0 pu1 pay", "win%d" % t)
-        if t > 0:
-            cp(T.xr[:, 0:128].indirect(T.au[:, 8:11]), T.pr[:, 144:192], "pr3 au", "xr")
+        if t == 0:
+            first_slots(pk)
+            acp(T.yb[:, 0:128], pb[3][:, 0:128], "", "p3 yb0")
         for a in range(4):
             tr(T.tb[0:32, a:512:4], T.win[32 * a:32 * a + 32, 224 * t:224 * t + 128], "win%d" % t, "tb%d" % a)
-            if t == 0 and a == 1:
-                slots(t, pos, pk)
         for b in range(4):
             tt(T.gcf[32 * b:32 * b + 32, :], T.tb[0:32, 128 * b:128 * b + 12], T.tb[0:32, 128 * b + 64:128 * b + 76], ADD, "tb0 tb1 tb2 tb3", "gc%d" % b)
         gc = "gc0 gc1 gc2 gc3"
@@ -498,7 +510,7 @@ def rank_program(g, core, T, topo):
             put_y(t - 1, "s")
             relist(t - 1)
         if t == R - 1:
-            spread(T.bm, 32, 64, "bm2 bm3")
+            cp(T.bu[:, 4 * t + 2:4 * t + 3], T.bt[:, 33 + 4 * t:34 + 4 * t], "bt%d" % (4 + t), "bo%d" % t)
             acp(T.yb[:, 128 * t:128 * t + 128], T.yb[:, 128 * t - 128:128 * t], "yb%d" % (t - 1), "yb%d" % t)
         for a in range(4):
             tt(T.fl[:, 65 * a:65 * a + 64], T.sg[:, 64 * a:64 * a + 64], T.thq[:, 64 * a:64 * a + 64], LT, "sg%d thq%d flb" % (a, a), "fl%d" % a)
@@ -507,28 +519,32 @@ def rank_program(g, core, T, topo):
             acp(T.csc[:, 0:16], T.ssc[:].indirect(pos), "ssc " + pk, "csc")
             kept(t, pos, pk)
         acp(T.ar[:, 64:128], tab[:].indirect(T.gu[:, 4:8]), tabs + " gu", "ar1")
-        if t == R - 1:
-            cp(T.bu[:, 4 * t + 2:4 * t + 3], T.bt[:, 32 + half:33 + half], bts, "bo%d" % t)
         scan(T.fs[:], T.rs65[:], T.fl[:], "rs65 stay fl0 fl1 fl2 fl3 flb", "fs")
         if t == R - 1:
             relist(t)
         cp(T.ru[:], T.fs[:, 64:260:65], "fs", "ru")
         if t + 1 < R:
             cp(T.csc[:].indirect(T.ru[:]), T.srt[:], "ru srt", "csc")
+            cp(T.cid[:, 16:144].indirect(T.ru[:]), T.ar[:, 64:128], "ru ar1", "cid")
             acp(T.ar[:, 128:192], tab[:, 0:1032].indirect(T.gu[:, 0:4]), tabs + " gu", "ar2")
-            if t > 0:
-                acp(T.yb[:, 128 * t:128 * t + 128], T.yb[:, 128 * t - 128:128 * t], "yb%d" % (t - 1), "yb%d" % t)
+            acp(T.bm[:, 17:272:2], T.bm[:, 0:16].indirect(cu[:, 16:24]), "bm0 z8", "bmb")
             cp(T.ssc[:].indirect(pos), T.csc[:, 0:16], "csc " + pk, "ssc")
             tt(T.dg[:], T.ssc[:], T.dm[:, 0:48], MUL, "ssc dm", "dg")
             scan(T.dgs[:], T.rs16[:, 0:48], T.dg[:], "rs16 dg", "dgs")
             for c in range(3):
                 act(T.sg[:, 64 * c:64 * c + 48], T.ssc[:], ACT.Sign, "ssc dgs", "sg%d" % c, bias=T.dgs[:, 16 * c + 15:16 * c + 16], scale=-1.0)
-            cp(T.cid[:, 16:144].indirect(T.ru[:]), T.ar[:, 64:128], "ru ar1", "cid")
+            cp(T.sid[:].indirect(pos), T.cid[:, 16:32], "cid " + pk, "sid")
             for c in range(3):
                 tt(T.ne[:, 48 * c:48 * c + 48], T.sg[:, 64 * c:64 * c + 48], T.thq[:, 64 * c:64 * c + 48], LT, "sg%d thq%d" % (c, c), "ne0 ne1 ne2 nf%d" % c if c == 0 else "nf%d" % c)
-            for d in range(2):
-                acp(T.bm[:, 16 * d:16 * d + 16], T.cid[:, 16:32], "cid", "bm%d" % d)
-            cp(T.sid[:].indirect(pos), T.cid[:, 16:32], "cid " + pk, "sid")
+            acp(T.bm[:, 16:272:2], T.cid[:, 16:32].indirect(cu[:, 16:24]), "cid z8", "bma")
+            spread(t)
+            if t > 0:
+                acp(T.yb[:, 128 * t:128 * t + 128], T.yb[:, 128 * t - 128:128 * t], "yb%d" % (t - 1), "yb%d" % t)
+            else:
+                lin(T.win[:, 224:672], tab[:, 0:448], 0.0, 0.0, tabs, "win1 win2")
+                for k in range(1, R):
+                    lin(T.idc[:, 32 * k:32 * k + 32], rows[:, 160:192], cf[:, 13:14], cf[:, 36 + k:37 + k], "rk lane kbm", "idc%d" % k)
+                acp(T.lf[:], tab[:, 0:128], "taba", "lf")
             scan(T.nr[:, 0:144], T.rs48[:], T.ne[:, 0:144], "rs48 nf0 nf1 nf2", "nr0 nr1 nr2")
             cp(T.ou[:, 0:3], T.nr[:, 47:144:48], "nr0", "ou")
             cp(T.srt[:, 16:64].indirect(T.ou[:, 0:3]), T.sid[:], "ou sid", "srt")
@@ -542,19 +558,21 @@ def rank_program(g, core, T, topo):
             dma("s", ps[t + 1][:, X0:KB[t + 1]], ps[t][:, X0:KB[t + 1]], pool(t), "pc%ds" % (t + 1))
     t = R - 1
     cp(T.cid[:, 16:144].indirect(T.ru[:]), T.ar[:, 64:128], "ru ar1", "cid")
+    tt(T.lr[:, 0:128], T.lf[:], T.dm[:], MUL, "lf dm", "lr0")
     cp(T.cid[:, 0:16], T.cid[:, 16:32], "cid", "cid0")
-    spread(T.cid, 0, 32, "cid cid0")
-    cp(T.bu[:, 4 * t:4 * t + 1], T.bt[:, half:half + 1], bts, "bn%d" % t)
+    for b in range(4):
+        tr(T.bt[32 * b:32 * b + 32, 0:32], T.cid[blk:blk + 32, 0:32], "cid cid0", "bt%d" % b)
+    cp(T.bu[:, 4 * t:4 * t + 1], T.bt[:, half:half + 1], "bt0 bt1 bt2 bt3", "bn%d" % t)
+    scan(T.lr[:, 128:256], T.rs16[:], T.lr[:, 0:128], "rs16 lr0", "lr1")
     new_columns(t)
     new_y(t)
-    tt(T.lr[:, 0:128], T.lf[:], T.dm[:], MUL, "lf dm", "lr0")
-    acp(T.yn[:], pb[3][:, 112:128], "", "p3 yn")
-    scan(T.lr[:, 128:256], T.rs16[:], T.lr[:, 0:128], "rs16 lr0", "lr1")
-    put_y(t, "s")
     cp(T.lu[:, 0:8], T.lr[:, 143:256:16], "lr1", "lu")
-    pick(T.oq[:], T.op[:], T.hq[:], T.hs[:], T.lu[:, 0:8], "hx h0q h0s h1q h1s h2q h2s lu", "o")
+    cp(T.oq[:].bitcast(dt.uint32), T.hq[:].bitcast(dt.uint32).indirect(T.lu[:, 0:8]), "hx h0q h1q h2q lu", "oq")
+    acp(T.op[:], T.hs[:].indirect(T.lu[:, 0:8]), "hx h0s h1s h2s lu", "os")
     dma("s", T.oc[:], T.oq[:].bitcast(U8), "oq", "")
+    cp(T.yn[:], pb[3][:, 112:128], "", "p3 yn")
     for k in range(4):
         dma("s" if k == 3 else "a", T.osc[4 * k:4 * k + 4, :], T.op[32 * k:32 * k + 4, :], "os", "")
+    put_y(t, "s")
     for tok in total.items():
         wait("g", tok)

from concourse.bass import DstId, RemoteDMATransfer
from concourse.mybir import dt, AluOpType, AxisListType, ActivationFunctionType

N, P, K, CAPP, R = 8, 128, 16, 8, 3
A = R * K
X0 = 16
X1 = X0 + N * K
KB = [X1 + N * (A - K) + 2 * N * K * t for t in range(R + 1)]
LOW = -1e29
C, S, F, H, U, I = "float8_e4m3fn_x4", "uint8", "float32", "bfloat16", "uint16", "int32"


def _sb(n, d):
    return ("sbuf", [128, n], d)


SCRATCH = {
    "xt": _sb(512, H), "ut": _sb(512, H), "u2t": _sb(1024, H), "kt": _sb(1024, H),
    "wq": _sb(1024, C), "wp": _sb(1024, S), "xq": _sb(128, C), "xs": _sb(128, S), "uq": _sb(128, C), "us": _sb(128, S),
    "urq": _sb(128, C), "urs": _sb(128, S), "u2q": _sb(256, C), "u2s": _sb(256, S),
    "sq": _sb(64, C), "sp": _sb(64, S), "fq": _sb(32, C), "fp": _sb(32, S), "fd": ("dram", [128, 1], F),
    "q1": _sb(KB[1], C), "s1": _sb(KB[1], S), "q2": _sb(KB[2], C), "s2": _sb(KB[2], S), "q3": _sb(KB[3], C), "s3": _sb(KB[3], S),
    "pq1": _sb(128, C), "ps1": _sb(128, S), "pq2": _sb(128, C), "ps2": _sb(128, S),
    "hq": _sb(P + A, C), "hs": _sb(P + A, S), "oq": _sb(128, C), "op": _sb(128, S),
    "da": ("dram", [N, 128, 1], F), "lx": _sb(64, U), "lxf": _sb(80, F),
    "tab": _sb(KB[3], F), "tabl": _sb(1032, F), "spool": _sb(KB[3], F),
    "ci": _sb(16, I), "cf": _sb(48, F), "cu": _sb(24, U), "rows": _sb(320, F),
    "thr": _sb(128, H), "thq": _sb(256, H), "dm": _sb(128, F), "rs16": _sb(128, F), "hm": _sb(40, F), "tm": _sb(66, H),
    "rs33": _sb(66, H), "rs65": _sb(260, H), "rs48": _sb(144, H), "one": _sb(48, H), "idc": _sb(96, F), "jfr": _sb(64, F),
    "oc48": _sb(160, F),
    "xg": _sb(16, F), "sg": _sb(256, H), "fl": _sb(260, H), "fs": _sb(260, H), "ob": _sb(32, H), "orow": _sb(128, H),
    "ne": _sb(384, H), "nr": _sb(384, H), "so": _sb(8, U), "xm": _sb(32, F), "plb": _sb(8, F), "mrow": _sb(96, F),
    "mst": _sb(208, F), "md": _sb(112, F), "me2": _sb(112, F), "mu": _sb(8, U), "mc": _sb(48, F), "ml": _sb(48, F),
    "ax": _sb(24, F), "au": _sb(24, U), "xr": _sb(192, F),
    "sid": _sb(48, F), "ssc": _sb(48, F), "smk": _sb(48, F),
    "cid": _sb(144, F), "csc": _sb(128, F), "cmk": _sb(128, F),
    "bits": _sb(40, F), "hz": _sb(40, F), "ku": _sb(4, U), "eqb": _sb(66, H), "eqm": _sb(66, H), "eqs": _sb(66, F),
    "sm": _sb(32, F), "pu": _sb(2, U), "c2a": _sb(32, F), "c2": _sb(32, F), "pay": _sb(32, F), "win": _sb(3 * 224, F),
    "tb": _sb(512, F), "gcf": _sb(12, F), "gu": _sb(8, U), "dd": _sb(6 * 192, F), "vu": _sb(4, U), "ru": _sb(4, U),
    "ar": _sb(192, F), "dg": _sb(48, F), "dgs": _sb(48, F), "ou": _sb(4, U), "srt": _sb(64, F), "tc": _sb(128, F),
    "po": _sb(8, U), "pr": _sb(48 * 4, F), "pou": _sb(4, U), "bm": _sb(16 + 256, F), "bt": _sb(48, F), "bu": _sb(16, U),
    "lr": _sb(256, H), "lf": _sb(128, F), "lu": _sb(16, U), "yb": _sb(384, F), "yn": _sb(16, F),
}
for _b in range(8):
    SCRATCH["pb%d" % _b] = ("psum", [128, 512], F)
SEMAPHORES = ["nv", "na", "nt", "ng", "sent", "in1", "in2", "in3", "in4", "hand", "hand2"] + ["d%d" % i for i in range(24)]

ADD, SUB, MUL, MAX, MIN = AluOpType.add, AluOpType.subtract, AluOpType.mult, AluOpType.max, AluOpType.min
GE, GT, LE, LT, EQ, NE = AluOpType.is_ge, AluOpType.is_gt, AluOpType.is_le, AluOpType.is_lt, AluOpType.is_equal, AluOpType.not_equal
AND = AluOpType.bitwise_and
ACT = ActivationFunctionType
U8 = dt.uint8


def _write(g, T, topo, src, dsts, pairs, lanes, sem):
    n = len(lanes) // len(pairs)
    ids = [DstId(rid=topo.addr(c)[0], pnc=topo.addr(c)[1]) for c in dsts]
    tf = []
    for i, (a, b) in enumerate(pairs):
        m = sum(1 << e for e in lanes[i * n:i * n + n])
        tf.append(RemoteDMATransfer(dst_ids=ids, dma_engine_mask=m, remote_sem=T.sem[sem], srcs=[a], dsts=[b] * len(ids)))
    g.remote_dma_fused(tf, local_sem=T.sem.sent)
    return n * len(pairs)


def _lanes(topo, src, dsts):
    return [e for e in topo.engines(src, dsts[0]) if all(e in topo.engines(src, c) for c in dsts)]


def _helpers(T, topo, home):
    r = T.rank_of(home)
    peers = [T.cores[(r + d) % N] for d in range(1, N)]
    near = [c for c in peers if topo.same_plane(topo.chip(home), topo.chip(c))]
    far = [c for c in peers if c not in near]
    free = sorted((c for c in topo.cores_of(home) if T.rank_of(c) is None), key=lambda c: topo.die(c) != topo.die(home))
    able = [c for c in free if all(topo.may_write(c, d) for d in far)]
    rest = [c for c in free if c not in able and all(topo.may_write(c, d) for d in near)]
    return [(able[0], far), (rest[0], near)], [(able[-1], far), (rest[-1], near)]


def _hand_on(g, core, T, topo):
    for home in T.cores:
        if topo.chip(home) != topo.chip(core):
            continue
        r = T.rank_of(home)
        a0, a1 = X0 + K * r, X1 + (A - K) * r
        off = _lanes(topo, home, [c for c in T.cores if c != home])
        spare = [e for e in topo.engines(home, core) if e not in off]
        first, later = _helpers(T, topo, home)
        for h, dsts in first + later:
            if h == core:
                lanes = _lanes(topo, h, dsts)
                if (h, dsts) in first:
                    g.wait_ge(T.sem.hand, len(off))
                    n = _write(g, T, topo, h, dsts, [(T.fd[:], T.da[r])], lanes, "in2")
                    g.wait_ge(T.sem.hand2, len(off))
                    n += _write(g, T, topo, h, dsts, [(T.fp[:, 0:16], T.s1[:, a0:a0 + 16])], lanes, "in1")
                else:
                    g.wait_ge(T.sem.hand, 2 * len(spare))
                    n = _write(g, T, topo, h, dsts, [(T.fq[:].bitcast(U8), T.q1[:, a1:a1 + 32].bitcast(U8))], lanes, "in3")
                    n += _write(g, T, topo, h, dsts, [(T.fp[:], T.s1[:, a1:a1 + 32])], lanes, "in3")
                g.wait_ge(T.sem.sent, n)


def rank_program(g, core, T, topo):
    me = T.rank_of(core)
    if me is None:
        _hand_on(g, core, T, topo)
        return
    eng = {"v": g.vector, "a": g.scalar, "t": g.tensor, "g": g, "s": g.sync}
    own = {"v": "nv", "a": "na", "t": "nt", "g": "ng"}
    total, seen, wrote, readers, ndma = {}, {q: {} for q in eng}, {}, {}, [0]

    def wait(q, tok):
        if seen[q].get(tok[0], 0) < tok[1] and not (q == "t" and tok[0] == "nt"):
            eng[q].wait_ge(T.sem[tok[0]], tok[1])
            seen[q][tok[0]] = tok[1]

    def ahead(q, r, w):
        need = {}
        for k in r.split() + w.split():
            for tok in ([wrote[k]] if k in wrote else []) + (readers.get(k, []) if k in w.split() else []):
                need[tok[0]] = max(need.get(tok[0], 0), tok[1])
        for tok in need.items():
            wait(q, tok)

    def behind(tok, r, w):
        for k in r.split():
            readers.setdefault(k, []).append(tok)
        for k in w.split():
            wrote[k], readers[k] = tok, []

    def op(q, call, r, w):
        ahead(q, r, w)
        s = own[q]
        total[s] = total.get(s, 0) + 1
        call(eng[q]).then_inc(T.sem[s], 1)
        behind((s, total[s]), r, w)

    def dma(q, out, in_, r, w):
        ahead(q, r, w)
        s = "d%d" % ndma[0]
        ndma[0] += 1
        total[s] = 16
        eng[q].dma_start(out, in_).then_inc(T.sem[s], 16)
        behind((s, 16), r, w)

    def ts(out, a, s1, o1, r, w, s2=None, o2=None):
        if o2 is None:
            op("v", lambda e: e.tensor_scalar(out, a, s1, None, o1), r, w)
        else:
            op("v", lambda e: e.tensor_scalar(out, a, s1, s2, o1, o2), r, w)

    def tt(out, a, b, o, r, w):
        op("v", lambda e: e.tensor_tensor(out, a, b, o), r, w)

    def cp(out, a, r, w):
        op("v", lambda e: e.tensor_copy(out, a), r, w)

    def fill(out, v, w):
        op("v", lambda e: e.memset(out, v), "", w)

    def scan(out, keep, a, r, w):
        op("v", lambda e: e.tensor_tensor_scan(out, keep, a, 0.0, MUL, ADD), r, w)

    def red(out, a, o, r, w, ab=False):
        op("v", lambda e: e.tensor_reduce(out, a, AxisListType.X, o, apply_absolute_value=ab), r, w)

    def tr(out, a, r, w):
        op("v", lambda e: e.transpose(out, a), r, w)

    def act(out, a, f, r, w, bias=0.0, scale=1.0, acc=None):
        op("a", lambda e: e.activation(out, a, f, bias=bias, scale=scale, accum_out=acc), r, w)

    def lin(out, a, scale, bias, r, w):
        act(out, a, ACT.Identity, r, w, bias=bias, scale=scale)

    def acp(out, a, r, w):
        op("a", lambda e: e.activation(out, a, ACT.Copy), r, w)

    def iota(out, pat, base, cm, w):
        op("g", lambda e: e.iota(out, pat, base, cm, allow_small_or_imprecise_dtypes=True), "", w)

    def quant(q, s, a, r, w):
        op("v", lambda e: e.quantize_mx(q, s, a), r, w)

    def mm(out, lq, ls, rq, rs, r, w, start=True, stop=True):
        op("t", lambda e: e.matmul_mx(out, lq, ls, rq, rs, start, stop), r, w)

    def pick(q, s, wq, ws, off, r, w):
        cp(q.bitcast(dt.uint32), wq.bitcast(dt.uint32).indirect(off), r, w + "q")
        acp(s, ws.indirect(off), r, w + "s")

    peers = [T.cores[(me + d) % N] for d in range(1, N)]
    assert all(topo.may_write(core, c) for c in peers)
    lanes = _lanes(topo, core, peers)
    first, hands = [[h for h, _d in hs] for hs in _helpers(T, topo, core)]
    spare = [e for e in _lanes(topo, core, hands) if e not in lanes]

    def send(dsts, pairs, use, sem, r):
        ahead("g", r, "")
        total["sent"] = total.get("sent", 0) + _write(g, T, topo, core, dsts, pairs, use, sem)

    for s, n in (("in1", 2), ("in2", 1), ("in3", 2), ("in4", 1)):
        total[s] = n * len(lanes) * len(peers)
        wrote[s] = (s, total[s])

    pb = [T["pb%d" % b] for b in range(8)]
    tab, cf, ci, cu, rows, sm = T.tab, T.cf, T.ci, T.cu, T.rows, T.sm
    a0, a1 = X0 + K * me, X1 + (A - K) * me
    tabs = "taba tabb"

    dma("s", T.xt[:], T.x[:], "", "xt")
    dma("a", T.ut[:], T.u[:], "", "ut")
    dma("s", T.wq[:].bitcast(U8), T.wc[:], "", "wq")
    dma("s", T.wp[:], T.ws[:], "", "wp")
    op("g", lambda e: e.iota(ci[:, 0:1], [[1, 1]], 0, 1), "", "ci0")
    iota(tab[:, 0:192], [[1, 192]], 0, 0, "taba")
    iota(rows[:, 0:128], [[0, 8], [1, 16]], 0, 0, "r16")
    iota(rows[:, 128:160], [[1, 2], [2, 16]], 0, 0, "rn")
    iota(rows[:, 160:192], [[128, 2], [1, 16]], 0, 0, "rk")
    iota(rows[:, 192:320], [[1, 16], [16, 8]], 0, 0, "rx")
    iota(tab[:, 192:KB[3]], [[1, KB[3] - 192]], 192, 0, "tabb")
    o48 = T.oc48
    fill(cu[:, 0:8], 0, "zo")
    fill(T.one[:], 1.0, "one")
    fill(T.hm[:], 2.0, "hm")
    fill(T.rs48[:], 1.0, "rs48")
    fill(o48[:], 0.0, "o48")
    fill(T.tm[:], 1.0, "tm")
    fill(T.rs33[:], 1.0, "rs33")
    fill(T.rs65[:], 1.0, "rs65")
    for i, m in enumerate((15, 112, 16)):
        ts(ci[:, i + 1:i + 2], ci[:, 0:1], m, AND, "ci0", "ci%d" % (i + 1))
    fill(T.hm[:, 0:40:10], 0.0, "hm")
    fill(T.rs48[:, 0:144:48], 0.0, "rs48")
    fill(o48[:, 0:16], 1.0, "o48")
    cp(cf[:, 0:4], ci[:, 0:4], "ci0 ci1 ci2 ci3", "cf")
    fill(T.rs33[:, 0:66:33], 0.0, "rs33")
    fill(T.rs65[:, 0:260:65], 0.0, "rs65")
    fill(o48[:, 64:96], 1.0, "o48")
    fill(T.lxf[:, 64:80], 0.0, "lxp")
    pcol, zcol = cf[:, 0:1], cf[:, 1:2]
    ts(T.thr[:], tab[:, 0:128], pcol, LT, "taba cf", "thr", 0.5, SUB)
    ts(cf[:, 8:12], tab[:, 0:64:16], zcol, ADD, "taba cf", "jc")
    jc = [cf[:, 8 + a:9 + a] for a in range(4)]
    ts(cf[:, 12:15], tab[:, 0:3], zcol, EQ, "taba cf", "lane")
    ts(cf[:, 20:22], tab[:, 0:2], zcol, ADD, "taba cf", "nn", zcol, ADD)
    lin(o48[:, 96:112], tab[:, 0:16], 1.0, float(a0), "taba o48", "o48a")
    lin(o48[:, 112:144], tab[:, 0:32], 1.0, float(a1), "taba o48", "o48b")
    lin(cf[:, 16:17], cf[:, 3:4], 0.5, 0.0, "cf", "e8")
    lin(cf[:, 17:18], cf[:, 3:4], 0.5, float(CAPP), "cf", "e16")
    lin(cf[:, 18:20], cf[:, 8:10], 1.0, 192.0, "jc", "dump")
    lin(cf[:, 32:35], tab[:, 0:3], 2.0 * N * K, cf[:, 2:3], "taba cf", "kb")
    lin(cf[:, 35:36], cf[:, 13:14], float(KB[0]), 0.0, "lane", "kb0")
    lin(cf[:, 36:39], cf[:, 32:35], cf[:, 13:14], cf[:, 35:36], "kb kb0 lane", "kbm")

    quant(T.uq[:], T.us[:], T.ut[:], "ut", "uq")
    quant(T.xq[:], T.xs[:], T.xt[:], "xt", "xq")
    pick(T.urq[:], T.urs[:], T.uq[:], T.us[:], cu[:, 0:8], "uq zo", "ur")
    mm(pb[0][:, 0:128], T.xq[:], T.xs[:], T.uq[:], T.us[:], "xq uq", "p0")
    mm(pb[1][:, 0:128], T.urq[:], T.urs[:], T.xq[:], T.xs[:], "xq urq urs", "p1")
    cp(T.xg[:, 0:1], pb[0][:, 0:1], "", "p0 xg")
    ts(T.xm[:, 0:10], pb[0][:, 4:14], 0.0, GT, "", "p0 xm0")
    act(T.sg[:, 0:128], pb[1][:, 0:128], ACT.Sign, "xg", "p1 sg0 sg1", bias=T.xg[:, 0:1], scale=-1.0)
    ts(T.tm[:, 1:33], rows[:, 128:160], cf[:, 20:21], LT, "rn nn tm", "tm0")
    scan(T.xm[:, 16:26], T.hm[:, 20:30], T.xm[:, 0:10], "hm xm0", "xm1")
    ts(T.tm[:, 34:66], rows[:, 128:160], cf[:, 21:22], LT, "rn nn tm", "tm1")
    ts(T.xm[:, 28:29], T.xm[:, 25:26], 1.0, ADD, "xm1", "xm2")
    send(first, [(T.xm[:, 28:29], T.fd[:])], lanes, "hand", "xm2")
    dma("s", T.da[me], T.xm[:, 28:29], "xm2", "da")
    for h in range(2):
        lin(T.u2t[:, 512 * h:512 * h + 512], T.ut[:], 0.0, 0.0, "ut", "u2%d" % h)
    tt(T.fl[:, 0:128], T.sg[:, 0:128], T.thr[:], LT, "sg0 sg1 thr", "fl0 fl1 fl2")
    red(T.xg[:, 1:2], T.fl[:, 0:128], ADD, "fl0", "xo")
    ts(T.ob[:], T.one[:, 0:32], T.xg[:, 1:2], MUL, "xo one", "ob")
    for a in range(4):
        tr(T.orow[0:32, 32 * a:32 * a + 32], T.ob[32 * a:32 * a + 32, :], "ob", "or%d" % a)
    orow = "or0 or1 or2 or3"

    def miss(c):
        ts(T.ne[0:32, 128 * c:128 * c + 128], T.orow[0:32, :], cf[0:32, 8 + c:9 + c], NE, orow + " jc", "ne%d" % c)

    def after(c):
        v = slice(128 * c, 128 * c + 128)
        scan(T.nr[0:32, v], T.ne[0:32, v], T.ne[0:32, v], "ne%d" % c, "nr%d" % c)

    miss(0)
    miss(1)
    after(0)
    miss(2)
    for b in range(4):
        ts(T.so[32 * b:32 * b + 32, 0:1], T.nr[0:32, 127:128], -1.0, MUL, "nr0", "so%d" % b, 127.0, ADD)
    so = "so0 so1 so2 so3"
    pick(T.sq[:, 0:16], T.sp[:, 0:16], T.xq[:], T.xs[:], T.so[:, 0:1], "xq " + so, "sa")
    send(first, [(T.sp[:, 0:16], T.fp[:, 0:16])], lanes, "hand2", "sas")
    send(peers, [(T.sq[:, 0:16].bitcast(U8), T.q1[:, a0:a0 + 16].bitcast(U8))], lanes, "in1", "saq")

    after(1)
    after(2)
    pick(T.q1[:, a0:a0 + 16], T.s1[:, a0:a0 + 16], T.xq[:], T.xs[:], T.so[:, 0:1], "xq " + so, "oa")
    for b in range(4):
        ts(T.so[32 * b:32 * b + 32, 2:4], T.nr[0:32, 255:384:128], -1.0, MUL, "nr1 nr2", "sp%d" % b, 127.0, ADD)
    sp = "sp0 sp1 sp2 sp3"
    cp(T.mu[:, 0:1], T.so[:, 0:1], so, "mu0")
    cp(T.mu[:, 1:3], T.so[:, 2:4], sp, "mu1")
    pick(T.sq[:, 16:48], T.sp[:, 16:48], T.xq[:], T.xs[:], T.so[:, 2:4], "xq " + sp, "sb")
    cp(T.mc[:, 0:3], T.mu[:, 0:3], "mu0 mu1", "mc")
    cp(T.mrow[:, 0:48], tab[:, 0:128].indirect(T.mu[:, 0:3]), "taba mu0 mu1", "mrow")
    pick(T.q1[:, a1:a1 + 32], T.s1[:, a1:a1 + 32], T.xq[:], T.xs[:], T.so[:, 2:4], "xq " + sp, "ob1")
    send(hands, [(T.sq[:, 16:48].bitcast(U8), T.fq[:].bitcast(U8))], spare, "hand", "sbq")
    send(hands, [(T.sp[:, 16:48], T.fp[:])], spare, "hand", "sbs")
    for c in range(3):
        ts(T.fl[:, 48 * c:48 * c + 48], T.mrow[:, 0:48], T.mc[:, c:c + 1], LT, "mrow mc", "fl%d" % c)
    acp(T.mrow[:, 48:96], rows[:, 192:320].indirect(T.mu[:, 0:3]), "rx mu0 mu1", "mrx")
    acp(T.mst[:, 96:112], rows[:, 192:320].indirect(T.mu[:, 0:1]), "rx mu0 mu1", "ms3")
    for h in range(2):
        for i in range(3):
            j = 128 * h + 10 * h + 9 - i
            acp(T.u2t[:, 4 * j:4 * j + 4], T.ut[:, 4 + 4 * i:8 + 4 * i], "ut u2%d" % h, "u2%d%d" % (h, i))
        j = 128 * h + 20 + 10 * h
        acp(T.u2t[:, 4 * j:4 * j + 40], T.ut[:, 16:56], "ut u2%d" % h, "u2%d3" % h)
    lin(T.win[:, 0:224], tab[:, 0:224], 0.0, 0.0, tabs, "win0")
    lin(T.tabl[:], tab[:, 0:1032], cf[:, 12:13], 0.0, tabs + " lane", "tabl")
    lin(T.idc[:, 0:32], rows[:, 160:192], cf[:, 13:14], cf[:, 36:37], "rk lane kbm", "idc0")
    ts(T.dm[:], rows[:, 0:128], zcol, EQ, "r16 cf", "dm")
    scan(T.fs[:, 0:144], T.rs48[:], T.fl[:, 0:144], "rs48 fl0 fl1 fl2", "fs")
    ts(T.rs16[:], rows[:, 0:128], 0.0, GT, "r16", "rs16")
    cp(T.mu[:, 4:7], T.fs[:, 47:144:48], "fs", "mu4")
    sl = T.mu[:, 4:7]
    cp(T.mst[:, 112:160].indirect(sl), o48[:, 0:48], "o48 mu4", "ms2")
    cp(T.mst[:, 0:48].indirect(sl), T.mrow[:, 48:96], "mrx mu4", "ms0")
    cp(T.mst[:, 48:96].indirect(sl), o48[:, 96:144], "o48a o48b mu4", "ms1")
    scan(T.ml[:], T.one[:], T.mst[:, 112:160], "one ms2", "ml")
    tt(T.md[:], T.mst[:, 0:112], T.dm[:, 0:112], MUL, "ms0 ms1 ms3 dm", "md")
    ts(T.mc[:], T.ml[:], zcol, LE, "ml cf", "mc")
    scan(T.me2[:], T.rs16[:, 0:112], T.md[:], "rs16 md", "me2")
    red(T.plb[:, 3:4], T.mc[:], ADD, "mc", "plb")
    cp(T.lx[:, 8 * me:8 * me + 3], T.me2[:, 15:48:16], "me2", "lx0")
    cp(T.lx[:, 8 * me + 4:8 * me + 8], T.me2[:, 63:112:16], "me2", "lx1")
    cp(T.lx[:, 8 * me + 3:8 * me + 4], T.plb[:, 3:4], "plb", "lx2")
    send(peers, [(T.lx[:, 8 * me:8 * me + 8], T.lx[:, 8 * me:8 * me + 8])], lanes, "in4", "lx0 lx1 lx2")
    dma("s", T.ax[:, 0:8], T.da[:], "da in2", "axa")
    quant(T.u2q[:], T.u2s[:], T.u2t[:], "u200 u201 u202 u203 u210 u211 u212 u213", "u2q")
    ts(T.lu[:, 8:10], tab[:, 0:129:128], pcol, ADD, "taba cf", "ko")
    ts(cu[:, 8:9], cf[:, 2:3], 0.5, MUL, "cf", "lo8", zcol, ADD)
    ts(cu[:, 16:24], tab[:, 0:8], 0.0, MUL, "taba cf", "z8", zcol, ADD)
    w00 = (T.wq[:, 0:128], T.wp[:, 0:128])

    pq, ps = [T.q1, T.q2, T.q3], [T.s1, T.s2, T.s3]
    blk, half = 32 * (me // 2), 16 * (me % 2)
    wrote["pc0q"], wrote["pc0s"] = wrote["ob1q"], wrote["ob1s"]

    def pool(t):
        return "in1 in3 oaq oas pc%dq pc%ds k%d0 k%d1" % (t, t, t, t)

    def spread(t):
        dma("s", T.bt[:, 32 + 4 * t:34 + 4 * t], T.bm[16 * me:16 * me + 1, 16:272], "bma bmb", "bt%d" % (4 + t))

    def new_columns(t):
        v = slice(P + K * t, P + K * t + K)
        pick(T.hq[:, v], T.hs[:, v], pq[t][:], ps[t][:], T.bu[:, 4 * t:4 * t + 1], pool(t) + " bn%d" % t, "h%d" % t)

    def new_y(t):
        v = slice(K * t + K, P + K * t + K)
        mm(pb[3][:, 0:128], w00[0], w00[1], T.hq[:, v], T.hs[:, v], "wq wp hx h0q h0s h1q h1s h2q h2s", "p3")

    def put_y(t, q):
        v = slice(128 * t, 128 * t + 128)
        cp(T.yb[:, v].indirect(T.bu[:, 4 * t + 2:4 * t + 3]), T.yn[:], "yn bo%d" % t, "yb%d" % t)
        dma(q, T.y[:, v], T.yb[:, v], "yb%d" % t, "")

    def relist(t):
        cp(T.lf[:].indirect(T.bu[:, 4 * t + 2:4 * t + 3]), tab[:, P + K * t:P + K * t + K], "taba bo%d" % t, "lf")

    def first_slots(pk):
        cp(T.au[:, 0:16], T.ax[:, 0:16], "axa axb", "au")
        cp(T.au[:, 16:20:2], T.ax[:, 11:16:4], "axb", pk)
        acp(T.xr[:, 0:128], tab[:, 0:1032].indirect(T.au[:, 0:8]), tabs + " au", "xr")
        acp(T.smk[:], T.xr[:, 0:128].indirect(T.au[:, 8:11]), "xr au", "smk")

    def kept(t, pos, pk):
        if t == 0:
            acp(T.sid[:], tab[:, 0:KB[0]].indirect(T.au[:, 12:15]), tabs + " au", "sid")
        acp(T.cid[:, 16:32], T.sid[:].indirect(pos), "sid " + pk, "cid")
        acp(T.cmk[:, 0:16], T.smk[:].indirect(pos), "smk " + pk, "cmk")
        acp(T.bm[:, 0:16], T.mst[:, 160:208].indirect(pos), "spl " + pk, "bm0")

    poss = [T.au[:, 16:17], T.pou[:, 0:1], T.pou[:, 2:3]]
    for t in range(R):
        kb, pos, pk = KB[t], poss[t], "pos%d" % t
        if t == 0:
            vq, vs, vr = T.q1[:, X0:X1], T.s1[:, X0:X1], "in1 oaq oas"
        else:
            vq, vs, vr = T["pq%d" % t][:], T["ps%d" % t][:], "v%dq v%ds" % (t, t)
        for i in range(8):
            mm(pb[i][:, 0:128], T.wq[:, 128 * i:128 * i + 128], T.wp[:, 128 * i:128 * i + 128], vq, vs, "wq wp " + vr, "p%d" % i)
        if t == 0:
            cp(T.mst[:, 160:208].indirect(sl), T.mrow[:, 0:48], "mrow mu4", "spl")
            fill(T.spool[:, 0:16], LOW, "spl0")
            for a in range(2):
                ts(T.thq[:, 64 * a:64 * a + 64], tab[:, 0:64], jc[a], LT, "taba jc", "thq%d" % a, 0.5, SUB)
        else:
            cp(T.pr[:, 0:48], o48[:, 0:48].indirect(T.ou[:, 0:3]), "o48 ou", "pr0")
            cp(T.cmk[:].indirect(T.ru[:]), T.ar[:, 128:192], "ru ar2", "cmk")
            scan(T.pr[:, 48:96], T.one[:], T.pr[:, 0:48], "one pr0", "pr1")
            cp(T.smk[:].indirect(poss[t - 1]), T.cmk[:, 0:16], "cmk pos%d" % (t - 1), "smk")
        for m in range(2):
            for b in range(4):
                i = 4 * m + b
                out = T.kt[:, 512 * m + b:512 * m + 512:4]
                if b == 3:
                    ts(out, pb[i][:, 0:128], 0.0, MAX, "", "p%d kt%d" % (i, i), 0.05, MUL)
                else:
                    act(out, pb[i][:, 0:128], ACT.Relu, "", "p%d kt%d" % (i, i), scale=0.05)
            v = slice(kb + 128 * m, kb + 128 * m + 128)
            quant(pq[t][:, v], ps[t][:, v], T.kt[:, 512 * m:512 * m + 512], " ".join("kt%d" % (4 * m + b) for b in range(4)), "k%d%d" % (t, m))
            w = slice(128 * m, 128 * m + 128)
            mm(pb[0][:, 0:128], pq[t][:, v], ps[t][:, v], T.u2q[:, w], T.u2s[:, w], "u2q k%d%d" % (t, m), "p0", m == 0, m == 1)
            if t == 0 and m == 0:
                for a in range(2, 4):
                    ts(T.thq[:, 64 * a:64 * a + 64], tab[:, 0:64], jc[a], LT, "taba jc", "thq%d" % a, 0.5, SUB)
            if t == 0 and m == 1:
                quant(T.hq[:, 0:128], T.hs[:, 0:128], T.xt[:], "xt", "hx")
            if t > 0 and m == 0:
                ts(T.pr[:, 96:144], T.pr[:, 48:96], zcol, LE, "pr1 cf", "pr2")
                red(T.pr[:, 144:145], T.pr[:, 96:144], ADD, "pr2", "pr3")
        v = slice(kb, kb + 256)
        mm(pb[1][:, 0:256], T.urq[:], T.urs[:], pq[t][:, v], ps[t][:, v], "urq urs k%d0 k%d1" % (t, t), "p1")
        if t > 0:
            cp(pos, T.pr[:, 144:145], "pr3", pk)
            cp(T.bu[:, 4 * t - 4:4 * t:2], T.bt[:, 28 + 4 * t:30 + 4 * t], "bt%d" % (3 + t), "bn%d bo%d" % (t - 1, t - 1))
            tt(T.pr[:, 144:192], o48[:, 48:96].indirect(T.ou[:, 0:3]), T.smk[:], MUL, "o48 ou smk", "pr3")
        else:
            mm(pb[3][:, 0:128], w00[0], w00[1], T.xq[:], T.xs[:], "wq wp xq", "p3")
        acp(T.spool[:, v], pb[1][:, 0:256], "", "p1 sk%d" % t)
        ts(T.bits[:], pb[0][:, 0:40], 0.0, GT, "", "p0 bits")
        if t > 0:
            cp(T.xr[:, 0:128].indirect(T.au[:, 8:11]), T.pr[:, 144:192], "pr3 au", "xr")
        scan(T.hz[:], T.hm[:], T.bits[:], "hm bits", "hz")
        ts(T.ku[:], T.hz[:, 9:40:10], 1.0, ADD, "hz", "ku")
        lin(T.eqb[:, 0:66:33], T.hz[:, 9:20:10], 16.0, cf[:, 16:17], "hz e8", "eq2")
        lin(T.c2a[:], T.spool[:, v].indirect(T.lu[:, 8:10]), cf[:, 14:15], 0.0, "sk%d ko lane" % t, "c2a")
        lin(sm[:, 0:2], T.hz[:, 9:20:10], 16.0, cf[:, 17:18], "hz e16", "lim")
        for h in range(2):
            ts(T.eqb[:, 33 * h + 1:33 * h + 33], tab[:, 0:16].indirect(T.ku[:, 0:2]), 1.0, SUB, "taba ku hz", "eq%d" % h, T.hz[:, 9 + 10 * h:10 + 10 * h], EQ)
        tt(T.eqm[:], T.eqb[:], T.tm[:], MUL, "eq0 eq1 eq2 tm0 tm1", "eqm")
        tt(T.c2[:], T.c2a[:], T.idc[:, 32 * t:32 * t + 32], ADD, "c2a idc%d" % t, "c2")
        scan(T.eqs[:], T.rs33[:], T.eqm[:], "rs33 eqm", "eqs")
        tt(T.pay[:], T.tabl[:].indirect(T.ku[:, 2:4]), T.c2[:], ADD, "tabl ku c2", "pay")
        tt(sm[:, 2:4], T.eqs[:, 32:66:33], sm[:, 0:2], GE, "eqs lim", "over")
        if t > 0:
            new_columns(t - 1)
            new_y(t - 1)
        else:
            lin(cf[:, 24:28:2], cf[:, 8:12:2], 1.0 / 256, 0.0, "jc", "jc1a")
            lin(cf[:, 25:28:2], cf[:, 9:12:2], 1.0 / 128, 1.0 / 256, "jc", "jc1b")
            lin(T.jfr[:], tab[:, 1:65], 1.0 / 128, 0.0, "taba", "jfr")
            lin(sm[:, 24:28:2], cf[:, 8:12:2], 1.0 / 256, 1.0 / 256, "jc", "hi0 hi2")
            lin(cf[:, 28:32], cf[:, 8:12], 1.0, 64.0, "jc", "j64")
        for h in range(2):
            ts(T.pu[:, h:h + 1], sm[:, 2 + h:3 + h], cf[:, 18 + h:19 + h], MUL, "over dump eqs", "pu%d" % h, T.eqs[:, 32 + 33 * h:33 + 33 * h], MAX)
        if t > 0:
            acp(T.csc[:, 0:16], T.ssc[:].indirect(pos), "ssc " + pk, "csc")
            kept(t, pos, pk)
            acp(T.yn[:], pb[3][:, 112:128], "", "p3 yn")
        else:
            cp(T.lxf[:, 0:64], T.lx[:], "in4 lx0 lx1 lx2", "lxf")
            acp(T.ax[:, 8:24], T.lxf[:].indirect(cu[:, 8:9]), "lxf lxp lo8", "axb")
        if t == R - 1:
            acp(T.bm[:, 17:272:2], T.bm[:, 0:16].indirect(cu[:, 16:24]), "bm0 z8", "bmb")
            spread(t)
        win = T.win[:, 224 * t:224 * t + 224]
        cp(win.indirect(T.pu[:]), T.pay[:], "pu0 pu1 pay", "win%d" % t)
        if t == 0:
            first_slots(pk)
            acp(T.yb[:, 0:128], pb[3][:, 0:128], "", "p3 yb0")
        for a in range(4):
            tr(T.tb[0:32, a:512:4], T.win[32 * a:32 * a + 32, 224 * t:224 * t + 128], "win%d" % t, "tb%d" % a)
        for b in range(4):
            tt(T.gcf[32 * b:32 * b + 32, :], T.tb[0:32, 128 * b:128 * b + 12], T.tb[0:32, 128 * b + 64:128 * b + 76], ADD, "tb0 tb1 tb2 tb3", "gc%d" % b)
        gc = "gc0 gc1 gc2 gc3"
        cp(T.gu[:], T.gcf[:, 0:8], gc, "gu")
        tt(sm[:, 4:8], T.gcf[:, 0:4], cf[:, 24:28], ADD, gc + " jc1a jc1b", "mid")
        if t == 0:
            cp(T.xr[:, 0:128].indirect(T.au[:, 18:19]), o48[:, 144:160], "o48 " + pk, "xr")
        tt(T.xr[:, 128:192], tab[:, 0:1032].indirect(T.gu[:, 0:4]), T.jfr[:], ADD, tabs + " gu jfr", "xa")
        if t == 0:
            mm(pb[2][:, 0:384], T.urq[:], T.urs[:], T.q1[:, X0:kb], T.s1[:, X0:kb], "urq urs in1 in3 oaq oas ob1q ob1s", "p2")
        for a in (3, 1):
            n = 144 + 16 * a
            act(T.dd[:, 192 * a:192 * a + n], T.xr[:, 0:n], ACT.Sign, "xr xa " + gc, "dd%d lo%d" % (a, a), bias=T.gcf[:, a:a + 1], scale=-1.0, acc=sm[:, 8 + a:9 + a])
            act(T.dd[:, 672 + 96 * a:672 + 96 * a + n], T.xr[:, 0:n], ACT.Sign, "xr xa mid", "de%d hi%d" % (a, a), bias=sm[:, 4 + a:5 + a], scale=-1.0, acc=sm[:, 24 + a:25 + a])
        for a in (2, 0):
            ts(T.dd[:, 192 * a:192 * a + 144 + 16 * a], T.xr[:, 0:144 + 16 * a], sm[:, 4 + a:5 + a], SUB, "xr xa mid", "dd%d" % a)
        for a in (2, 0):
            red(sm[:, 8 + a:9 + a], T.dd[:, 192 * a:192 * a + 144 + 16 * a], MIN, "dd%d" % a, "lo%d" % a, ab=True)
        for a in (2, 3, 0, 1):
            ts(T.vu[:, a:a + 1], sm[:, 8 + a:9 + a], sm[:, 24 + a:25 + a], GE, "lo%d hi%d " % (a, a) + gc, "vu%d" % a, T.gcf[:, 4 + a:5 + a], MUL)
        if t == 0:
            acp(T.spool[:, X0:kb], pb[2][:, 0:384], "", "p2 spx")
        ends = "lo0 lo1 lo2 lo3 hi0 hi1 hi2 hi3"
        tt(sm[:, 12:16], sm[:, 8:12], sm[:, 24:28], LT, ends, "fall")
        acp(T.srt[:], T.spool[:, 0:kb + 256].indirect(T.vu[:]), "spl0 spx sk0 sk1 sk2 vu0 vu1 vu2 vu3", "srt srt0")
        tt(T.rs65[:, 64:260:65], sm[:, 8:12], sm[:, 24:28], GE, ends + " rs65", "stay")
        tt(T.fl[:, 64:260:65], sm[:, 12:16], cf[:, 28:32], MUL, "fall j64", "fl0 fl1 fl2 fl3 flb")
        for a in range(4):
            act(T.sg[:, 64 * a:64 * a + 64], T.srt[:], ACT.Sign, "srt " + gc, "sg%d" % a, bias=T.gcf[:, 8 + a:9 + a], scale=-1.0)
        if t > 0:
            put_y(t - 1, "s")
            relist(t - 1)
        if t == R - 1:
            cp(T.bu[:, 4 * t + 2:4 * t + 3], T.bt[:, 33 + 4 * t:34 + 4 * t], "bt%d" % (4 + t), "bo%d" % t)
            acp(T.yb[:, 128 * t:128 * t + 128], T.yb[:, 128 * t - 128:128 * t], "yb%d" % (t - 1), "yb%d" % t)
        for a in range(4):
            tt(T.fl[:, 65 * a:65 * a + 64], T.sg[:, 64 * a:64 * a + 64], T.thq[:, 64 * a:64 * a + 64], LT, "sg%d thq%d flb" % (a, a), "fl%d" % a)
        if t == 0:
            acp(T.ssc[:], T.spool[:, 0:kb].indirect(T.au[:, 12:15]), "spl0 spx au", "ssc")
            acp(T.csc[:, 0:16], T.ssc[:].indirect(pos), "ssc " + pk, "csc")
            kept(t, pos, pk)
        acp(T.ar[:, 64:128], tab[:].indirect(T.gu[:, 4:8]), tabs + " gu", "ar1")
        scan(T.fs[:], T.rs65[:], T.fl[:], "rs65 stay fl0 fl1 fl2 fl3 flb", "fs")
        if t == R - 1:
            relist(t)
        cp(T.ru[:], T.fs[:, 64:260:65], "fs", "ru")
        if t + 1 < R:
            cp(T.csc[:].indirect(T.ru[:]), T.srt[:], "ru srt", "csc")
            cp(T.cid[:, 16:144].indirect(T.ru[:]), T.ar[:, 64:128], "ru ar1", "cid")
            acp(T.ar[:, 128:192], tab[:, 0:1032].indirect(T.gu[:, 0:4]), tabs + " gu", "ar2")
            acp(T.bm[:, 17:272:2], T.bm[:, 0:16].indirect(cu[:, 16:24]), "bm0 z8", "bmb")
            cp(T.ssc[:].indirect(pos), T.csc[:, 0:16], "csc " + pk, "ssc")
            tt(T.dg[:], T.ssc[:], T.dm[:, 0:48], MUL, "ssc dm", "dg")
            scan(T.dgs[:], T.rs16[:, 0:48], T.dg[:], "rs16 dg", "dgs")
            for c in range(3):
                act(T.sg[:, 64 * c:64 * c + 48], T.ssc[:], ACT.Sign, "ssc dgs", "sg%d" % c, bias=T.dgs[:, 16 * c + 15:16 * c + 16], scale=-1.0)
            cp(T.sid[:].indirect(pos), T.cid[:, 16:32], "cid " + pk, "sid")
            for c in range(3):
                tt(T.ne[:, 48 * c:48 * c + 48], T.sg[:, 64 * c:64 * c + 48], T.thq[:, 64 * c:64 * c + 48], LT, "sg%d thq%d" % (c, c), "ne0 ne1 ne2 nf%d" % c if c == 0 else "nf%d" % c)
            acp(T.bm[:, 16:272:2], T.cid[:, 16:32].indirect(cu[:, 16:24]), "cid z8", "bma")
            spread(t)
            if t > 0:
                acp(T.yb[:, 128 * t:128 * t + 128], T.yb[:, 128 * t - 128:128 * t], "yb%d" % (t - 1), "yb%d" % t)
            else:
                lin(T.win[:, 224:672], tab[:, 0:448], 0.0, 0.0, tabs, "win1 win2")
                for k in range(1, R):
                    lin(T.idc[:, 32 * k:32 * k + 32], rows[:, 160:192], cf[:, 13:14], cf[:, 36 + k:37 + k], "rk lane kbm", "idc%d" % k)
                acp(T.lf[:], tab[:, 0:128], "taba", "lf")
            scan(T.nr[:, 0:144], T.rs48[:], T.ne[:, 0:144], "rs48 nf0 nf1 nf2", "nr0 nr1 nr2")
            cp(T.ou[:, 0:3], T.nr[:, 47:144:48], "nr0", "ou")
            cp(T.srt[:, 16:64].indirect(T.ou[:, 0:3]), T.sid[:], "ou sid", "srt")
            cp(T.srt[:, 0:16], T.srt[:, 16:32], "srt", "srt0")
            for a in range(4):
                tr(T.tc[0:32, 32 * a:32 * a + 32], T.srt[32 * a:32 * a + 32, 0:32], "srt srt0", "tc%d" % a)
            for b in range(4):
                cp(T.po[32 * b:32 * b + 32, :], T.tc[0:32, 0:128:16], "tc0 tc1 tc2 tc3", "po%d" % b)
            pick(T["pq%d" % (t + 1)][:], T["ps%d" % (t + 1)][:], pq[t][:], ps[t][:], T.po[:], pool(t) + " po0 po1 po2 po3", "v%d" % (t + 1))
            dma("s", pq[t + 1][:, X0:KB[t + 1]].bitcast(U8), pq[t][:, X0:KB[t + 1]].bitcast(U8), pool(t), "pc%dq" % (t + 1))
            dma("s", ps[t + 1][:, X0:KB[t + 1]], ps[t][:, X0:KB[t + 1]], pool(t), "pc%ds" % (t + 1))
    t = R - 1
    cp(T.cid[:, 16:144].indirect(T.ru[:]), T.ar[:, 64:128], "ru ar1", "cid")
    tt(T.lr[:, 0:128], T.lf[:], T.dm[:], MUL, "lf dm", "lr0")
    cp(T.cid[:, 0:16], T.cid[:, 16:32], "cid", "cid0")
    for b in range(4):
        tr(T.bt[32 * b:32 * b + 32, 0:32], T.cid[blk:blk + 32, 0:32], "cid cid0", "bt%d" % b)
    cp(T.bu[:, 4 * t:4 * t + 1], T.bt[:, half:half + 1], "bt0 bt1 bt2 bt3", "bn%d" % t)
    scan(T.lr[:, 128:256], T.rs16[:], T.lr[:, 0:128], "rs16 lr0", "lr1")
    new_columns(t)
    new_y(t)
    cp(T.lu[:, 0:8], T.lr[:, 143:256:16], "lr1", "lu")
    cp(T.oq[:].bitcast(dt.uint32), T.hq[:].bitcast(dt.uint32).indirect(T.lu[:, 0:8]), "hx h0q h1q h2q lu", "oq")
    acp(T.op[:], T.hs[:].indirect(T.lu[:, 0:8]), "hx h0s h1s h2s lu", "os")
    dma("s", T.oc[:], T.oq[:].bitcast(U8), "oq", "")
    cp(T.yn[:], pb[3][:, 112:128], "", "p3 yn")
    for k in range(4):
        dma("s" if k == 3 else "a", T.osc[4 * k:4 * k + 4, :], T.op[32 * k:32 * k + 4, :], "os", "")
    put_y(t, "s")
    for tok in total.items():
        wait("g", tok)
